import numpy as np
import ml_dtypes


def mxq(x, axis, fmt="e4m3"):
    dtype, down = {"e4m3": (ml_dtypes.float8_e4m3fn, 7), "e5m2": (ml_dtypes.float8_e5m2, 14)}[fmt]
    v = np.moveaxis(np.asarray(x, np.float32).astype(ml_dtypes.bfloat16).astype(np.float64), axis, -1)
    blocks = v.reshape(v.shape[:-1] + (-1, 32))
    amax = np.abs(blocks).max(-1, keepdims=True)
    byte = np.maximum(np.where(amax > 0, np.frexp(amax)[1] - 1 + 127, 0) - down, 1)
    scale = np.exp2(byte - 127.0)
    codes = (blocks / scale).astype(np.float32).astype(dtype).astype(np.float64)
    return np.moveaxis((codes * scale).reshape(v.shape), -1, axis)


WIDE = False


def mx_kscale(k):
    if not WIDE:
        return np.ones(k)
    levels = np.array([18, -18])
    if k % 512:
        return np.exp2(np.random.permutation(np.resize(levels, k // 32))).repeat(32)
    a = np.empty((k // 512, 16))
    for p in range(k // 512):
        a[p, :8] = np.random.permutation(np.resize(levels, 8))
        for g in range(8):
            far = levels[np.abs(levels - a[p, g]) >= 10]
            a[p, g + 8] = far[np.random.randint(len(far))]
    return np.exp2(a.ravel()).repeat(32)


def f64(x):
    return np.asarray(x).astype(np.float64)


def striped(idx):
    return np.tile(np.asarray(idx).reshape(-1, 16).T, (8, 1)).astype(np.uint16)


def unstriped(offs):
    return offs[:16].T.reshape(-1).astype(np.int64)


E2M1 = np.array([0.0, 0.5, 1.0, 1.5, 2.0, 3.0, 4.0, 6.0, -0.0, -0.5, -1.0, -1.5, -2.0, -3.0, -4.0, -6.0])


def pack_weight(w, fmt):
    k, n = w.shape
    w = f64(np.asarray(w, np.float32).astype(ml_dtypes.bfloat16)).reshape(k // 32, 32, n)
    amax = np.abs(w).max(1)
    if fmt == "e4m3":
        byte = np.frexp(amax)[1] - 1 + 127 - 7
    else:
        mant, ex = np.frexp(amax / 6.0)
        byte = np.where(mant > 0.5, ex, ex - 1) + 127
    byte = np.clip(np.where(amax > 0, byte, 1), 1, 254)
    scaled = (w * np.exp2(127.0 - byte)[:, None, :]).reshape(k, n).astype(np.float32)
    by_word = np.ascontiguousarray(scaled.reshape(k // 512, 128, 4, n).transpose(0, 1, 3, 2))
    if fmt == "e4m3":
        words = by_word.astype(ml_dtypes.float8_e4m3fn).view(np.uint8)
    else:
        c = by_word.astype(ml_dtypes.float4_e2m1fn).view(np.uint8) & 0xF
        words = (c[..., 0::2] | (c[..., 1::2] << 4)).reshape(k // 512, 128, 2 * n)
    return np.ascontiguousarray(words), np.ascontiguousarray(byte.astype(np.uint8).reshape(k // 512, 16, n))


def unpack_weight(words, scales, fmt):
    g, _, n = scales.shape
    words = np.ascontiguousarray(words).reshape(g, 128, n, -1)
    if fmt == "e4m3":
        vals = words.view(ml_dtypes.float8_e4m3fn).astype(np.float64)
    else:
        nib = np.empty((g, 128, n, 4), np.uint8)
        nib[..., 0::2] = words & 0xF
        nib[..., 1::2] = words >> 4
        vals = E2M1[nib]
    vals = vals * np.repeat(np.exp2(scales.astype(np.float64) - 127.0), 8, axis=1)[..., None]
    return vals.transpose(0, 1, 3, 2).reshape(g * 512, n)


T, C, D, DV = 512, 512, 512, 512
BETA = 0.25


def setup_inputs():
    n = np.random.standard_normal
    grid = lambda v: np.clip(np.round(v * 16) / 16, -4, 4)
    v = mx_kscale(DV)[:, None]
    wp = pack_weight(n((DV, D)) / np.sqrt(DV) / v, "e2m1")
    return {
        "zT": (grid(n((DV, T))) * v).astype(np.float32),
        "cb": (grid(n((DV, C))) * v).astype(np.float32),
        "cb2": (grid(0.5 * n((DV, C))) * v).astype(np.float32),
        "w_words": wp[0],
        "w_scales": wp[1],
        "offs": striped(np.random.randint(0, C, T)),
        "offs2": striped(np.random.randint(0, C, T)),
    }


def reference(zT, cb, cb2, w_words, w_scales, offs, offs2):
    e = f64(zT) - f64(cb)[:, unstriped(offs)] - f64(cb2)[:, unstriped(offs2)]
    g = BETA * e
    return unpack_weight(w_words, w_scales, "e2m1").T @ mxq(g, 0, "e5m2")

@@ -1,0 +1,143 @@
+from contextlib import ExitStack
+
+import concourse.mybir as mybir
+
+N_FEAT, T, C, D = 512, 512, 512, 512
+BETA = 0.25
+FLOPS = 2 * N_FEAT * D * T
+
+F32 = mybir.dt.float32
+BF16 = mybir.dt.bfloat16
+I32 = mybir.dt.int32
+U32 = mybir.dt.uint32
+U16 = mybir.dt.uint16
+U8 = mybir.dt.uint8
+E5M2X4 = mybir.dt.float8_e5m2_x4
+E2M1X4 = mybir.dt.float4_e2m1fn_x4
+SUBTRACT = mybir.AluOpType.subtract
+ADD = mybir.AluOpType.add
+COPY = mybir.ActivationFunctionType.Copy
+
+P = 128
+LANES = 4
+PER_COLUMN = 16
+CHUNKS = ((0, 256), (256, 384), (384, 448), (448, 512))
+
+
+def tile_attend_gvq_r_x_kernel(tc, zT, cb, cb2, w_words, w_scales, offs, offs2, out):
+    nc = tc.nc
+    z_planes = zT.rearrange("(p j) t -> p j t", j=LANES)
+    cb_planes = cb.rearrange("(p j) c -> p j c", j=LANES)
+    cb2_planes = cb2.rearrange("(p j) c -> p j c", j=LANES)
+
+    with ExitStack() as ctx:
+        keep = ctx.enter_context(tc.tile_pool(name="keep", bufs=1))
+        psum = ctx.enter_context(tc.psum_pool(name="psum", bufs=1))
+
+        code = keep.tile([P, T // PER_COLUMN], U16, name="code")
+        code2 = keep.tile([P, T // PER_COLUMN], U16, name="code2")
+        book = [keep.tile([P, C], F32, name="book%d" % j) for j in range(LANES)]
+        book2 = [keep.tile([P, C], F32, name="book2_%d" % j) for j in range(LANES)]
+        w_codes = keep.tile([P, 2 * D], U8, name="w_codes", align_bytes=64)
+        w_exps = keep.tile([P, D], U8, name="w_exps", align_bytes=64)
+        g_codes = keep.tile([P, T], U32, name="g_codes", align_bytes=64)
+        g_exps = keep.tile([P, T], U8, name="g_exps", align_bytes=64)
+
+        z_pieces = []
+
+        def load_z(queue, j0, j1, t0, t1):
+            piece = keep.tile([P, j1 - j0, t1 - t0], F32, name="z_%d_%d" % (j0, t0))
+            queue.dma_start(out=piece[:], in_=z_planes[:, j0:j1, t0:t1])
+            z_pieces.append((j0, j1, t0, t1, piece))
+
+        def z_of(j, t0, t1):
+            j0, a0, piece = [(j0, a0, piece) for j0, j1, a0, a1, piece in z_pieces if j0 <= j < j1 and a0 <= t0 and t1 <= a1][0]
+            return piece[:, j - j0, t0 - a0 : t1 - a0]
+
+        nc.gpsimd.memset(w_exps[:].bitcast(U32), 0)
+
+        nc.sync.dma_start(out=book[0][:], in_=cb_planes[:, 0, :])
+        nc.sync.dma_start(code[:], offs)
+        load_z(nc.scalar, 0, 1, 0, 128)
+        load_z(nc.sync, 0, 1, 128, 384)
+        nc.sync.dma_start(out=book2[0][:], in_=cb2_planes[:, 0, :])
+        nc.sync.dma_start(code2[:], offs2)
+        for j in range(1, LANES):
+            nc.sync.dma_start(out=book[j][:], in_=cb_planes[:, j, :])
+            load_z(nc.sync, j, j + 1, 0, 384 if j < 2 else 256)
+            nc.sync.dma_start(out=book2[j][:], in_=cb2_planes[:, j, :])
+        load_z(nc.sync, 2, 4, 256, 384)
+        load_z(nc.sync, 0, 4, 384, 512)
+        nc.sync.dma_start(out=w_codes[:].bitcast(I32), in_=w_words[0].bitcast(I32))
+        for q in range(4):
+            nc.sync.dma_start(
+                out=w_exps[32 * q : 32 * q + 4, :].bitcast(I32),
+                in_=w_scales[0, 4 * q : 4 * q + 4, :].bitcast(I32),
+            )
+
+        neg_e = [keep.tile([P, LANES, t1 - t0], F32, name="neg_e%d" % t0) for t0, t1 in CHUNKS]
+        g_bf = [keep.tile([P, t1 - t0, LANES], BF16, name="g_bf%d" % t0, align_bytes=64) for t0, t1 in CHUNKS]
+        partial = {}
+
+        def first_lookup(j, t0, t1):
+            part = keep.tile([P, t1 - t0], F32, name="part_%d_%d" % (j, t0))
+            window = book[j][:].indirect(code[:, t0 // PER_COLUMN : t1 // PER_COLUMN])
+            nc.vector.tensor_tensor(part[:], window, z_of(j, t0, t1), SUBTRACT)
+            partial[(j, t0)] = part
+
+        def second_lookup(j, t0, t1):
+            c = [i for i, (a0, a1) in enumerate(CHUNKS) if a0 <= t0 and t1 <= a1][0]
+            a0 = CHUNKS[c][0]
+            window = book2[j][:].indirect(code2[:, t0 // PER_COLUMN : t1 // PER_COLUMN])
+            nc.vector.tensor_tensor(neg_e[c][:, j, t0 - a0 : t1 - a0], window, partial[(j, t0)][:], ADD)
+
+        def interleave(c):
+            nc.scalar.activation(
+                out=g_bf[c][:].rearrange("p (s i) j -> p s j i", i=4),
+                in_=neg_e[c][:].rearrange("p j (s i) -> p s j i", i=4),
+                func=COPY,
+                scale=-BETA,
+            )
+
+        def quantise(c):
+            t0, t1 = CHUNKS[c]
+            nc.vector.quantize_mx(
+                out=g_codes[:, t0:t1].bitcast(E5M2X4),
+                scales=g_exps[:, t0:t1],
+                in_=g_bf[c][:].rearrange("p t j -> p (t j)"),
+            )
+
+        early = {0: ((0, 128), (128, 256), (256, 384)), 1: ((0, 256), (256, 384)), 2: ((0, 128), (128, 256)), 3: ((0, 128), (128, 256))}
+        for j in range(LANES):
+            for t0, t1 in early[j]:
+                first_lookup(j, t0, t1)
+            for t0, t1 in early[j]:
+                second_lookup(j, t0, t1)
+        interleave(0)
+        for c, planes in ((1, (2, 3)), (2, (0, 1, 2, 3)), (3, (0, 1, 2, 3))):
+            t0, t1 = CHUNKS[c]
+            for j in planes:
+                first_lookup(j, t0, t1)
+            for j in planes:
+                second_lookup(j, t0, t1)
+            interleave(c)
+        for c in range(len(CHUNKS)):
+            quantise(c)
+
+        for m in range(D // P):
+            acc = psum.tile([P, T], F32, name="acc%d" % m)
+            nc.tensor.matmul_mx(
+                out=acc[:],
+                lhsT=w_codes[:, 2 * P * m : 2 * P * (m + 1)].bitcast(E2M1X4),
+                lhsT_scale=w_exps[:, P * m : P * (m + 1)],
+                rhs=g_codes[:].bitcast(E5M2X4),
+                rhs_scale=g_exps[:],
+                start=True,
+                stop=True,
+            )
+            result = keep.tile([P, T], F32, name="result%d" % m)
+            if m % 2 == 0:
+                nc.scalar.copy(out=result[:], in_=acc[:])
+            else:
+                nc.vector.tensor_copy(out=result[:], in_=acc[:])
+            nc.sync.dma_start(out=out[P * m : P * (m + 1), :], in_=result[:])

@@ -1,6 +1,7 @@
 from contextlib import ExitStack
 
 import concourse.mybir as mybir
+from concourse.masks import make_identity
 
 N_FEAT, T, C, D = 512, 512, 512, 512
 BETA = 0.25
@@ -21,7 +22,8 @@ COPY = mybir.ActivationFunctionType.Copy
 P = 128
 LANES = 4
 PER_COLUMN = 16
-CHUNKS = ((0, 256), (256, 384), (384, 448), (448, 512))
+MAIN = 384
+MULT = mybir.AluOpType.mult
 
 
 def tile_attend_gvq_r_x_kernel(tc, zT, cb, cb2, w_words, w_scales, offs, offs2, out):
@@ -54,20 +56,28 @@ def tile_attend_gvq_r_x_kernel(tc, zT, cb, cb2, w_words, w_scales, offs, offs2, 
             j0, a0, piece = [(j0, a0, piece) for j0, j1, a0, a1, piece in z_pieces if j0 <= j < j1 and a0 <= t0 and t1 <= a1][0]
             return piece[:, j - j0, t0 - a0 : t1 - a0]
 
+        identity = keep.tile([P, P], F32, name="identity")
         nc.gpsimd.memset(w_exps[:].bitcast(U32), 0)
+        nc.gpsimd.memset(g_codes[:, MAIN:T], 0)
+        nc.gpsimd.memset(g_exps[:, MAIN:T].bitcast(U32), 0)
+        make_identity(nc, identity[:])
 
         nc.sync.dma_start(out=book[0][:], in_=cb_planes[:, 0, :])
         nc.sync.dma_start(code[:], offs)
-        load_z(nc.scalar, 0, 1, 0, 128)
-        load_z(nc.sync, 0, 1, 128, 384)
+        load_z(nc.scalar, 0, 1, 0, 192)
+        load_z(nc.sync, 0, 1, 192, MAIN)
         nc.sync.dma_start(out=book2[0][:], in_=cb2_planes[:, 0, :])
         nc.sync.dma_start(code2[:], offs2)
-        for j in range(1, LANES):
-            nc.sync.dma_start(out=book[j][:], in_=cb_planes[:, j, :])
-            load_z(nc.sync, j, j + 1, 0, 384 if j < 2 else 256)
+        nc.sync.dma_start(out=book[1][:], in_=cb_planes[:, 1, :])
+        load_z(nc.sync, 1, 2, 0, MAIN)
+        nc.sync.dma_start(out=book2[1][:], in_=cb2_planes[:, 1, :])
+        nc.sync.dma_start(out=book[2][:], in_=cb_planes[:, 2, :])
+        load_z(nc.sync, 2, 4, 0, 256)
+        nc.sync.dma_start(out=book[3][:], in_=cb_planes[:, 3, :])
+        for j in (2, 3):
             nc.sync.dma_start(out=book2[j][:], in_=cb2_planes[:, j, :])
-        load_z(nc.sync, 2, 4, 256, 384)
-        load_z(nc.sync, 0, 4, 384, 512)
+        load_z(nc.sync, 2, 4, 256, MAIN)
+        load_z(nc.sync, 0, 4, MAIN, T)
         nc.sync.dma_start(out=w_codes[:].bitcast(I32), in_=w_words[0].bitcast(I32))
         for q in range(4):
             nc.sync.dma_start(
@@ -75,57 +85,45 @@ def tile_attend_gvq_r_x_kernel(tc, zT, cb, cb2, w_words, w_scales, offs, offs2, 
                 in_=w_scales[0, 4 * q : 4 * q + 4, :].bitcast(I32),
             )
 
-        neg_e = [keep.tile([P, LANES, t1 - t0], F32, name="neg_e%d" % t0) for t0, t1 in CHUNKS]
-        g_bf = [keep.tile([P, t1 - t0, LANES], BF16, name="g_bf%d" % t0, align_bytes=64) for t0, t1 in CHUNKS]
-        partial = {}
-
-        def first_lookup(j, t0, t1):
-            part = keep.tile([P, t1 - t0], F32, name="part_%d_%d" % (j, t0))
+        def first_lookup(j, t0, t1, part):
             window = book[j][:].indirect(code[:, t0 // PER_COLUMN : t1 // PER_COLUMN])
-            nc.vector.tensor_tensor(part[:], window, z_of(j, t0, t1), SUBTRACT)
-            partial[(j, t0)] = part
+            nc.vector.tensor_tensor(part, window, z_of(j, t0, t1), SUBTRACT)
 
-        def second_lookup(j, t0, t1):
-            c = [i for i, (a0, a1) in enumerate(CHUNKS) if a0 <= t0 and t1 <= a1][0]
-            a0 = CHUNKS[c][0]
+        def second_lookup(j, t0, t1, part, neg):
             window = book2[j][:].indirect(code2[:, t0 // PER_COLUMN : t1 // PER_COLUMN])
-            nc.vector.tensor_tensor(neg_e[c][:, j, t0 - a0 : t1 - a0], window, partial[(j, t0)][:], ADD)
+            nc.vector.tensor_tensor(neg, window, part, ADD)
 
-        def interleave(c):
-            nc.scalar.activation(
-                out=g_bf[c][:].rearrange("p (s i) j -> p s j i", i=4),
-                in_=neg_e[c][:].rearrange("p j (s i) -> p s j i", i=4),
-                func=COPY,
-                scale=-BETA,
-            )
+        def woven(g_tile):
+            return g_tile.rearrange("p (s i) j -> p s j i", i=4)
 
-        def quantise(c):
-            t0, t1 = CHUNKS[c]
+        def by_lane(neg):
+            return neg.rearrange("p j (s i) -> p s j i", i=4)
+
+        part = [keep.tile([P, MAIN], F32, name="part%d" % j) for j in range(LANES)]
+        neg_e = keep.tile([P, LANES, MAIN], F32, name="neg_e", tag="stage")
+        for j in (0, 1):
+            for t0, t1 in ((0, 192), (192, MAIN)):
+                first_lookup(j, t0, t1, part[j][:, t0:t1])
+            for t0, t1 in ((0, 192), (192, MAIN)):
+                second_lookup(j, t0, t1, part[j][:, t0:t1], neg_e[:, j, t0:t1])
+        main_bf = []
+        for t0, t1 in ((0, 256), (256, MAIN)):
+            for j in (2, 3):
+                first_lookup(j, t0, t1, part[j][:, t0:t1])
+            for j in (2, 3):
+                second_lookup(j, t0, t1, part[j][:, t0:t1], neg_e[:, j, t0:t1])
+            g_bf = keep.tile([P, t1 - t0, LANES], BF16, name="g_bf%d" % t0, align_bytes=64)
+            nc.scalar.activation(out=woven(g_bf[:]), in_=by_lane(neg_e[:, :, t0:t1]), func=COPY, scale=-BETA)
+            main_bf.append((t0, t1, g_bf))
+        for t0, t1, g_bf in main_bf:
             nc.vector.quantize_mx(
                 out=g_codes[:, t0:t1].bitcast(E5M2X4),
                 scales=g_exps[:, t0:t1],
-                in_=g_bf[c][:].rearrange("p t j -> p (t j)"),
+                in_=g_bf[:].rearrange("p t j -> p (t j)"),
             )
 
-        early = {0: ((0, 128), (128, 256), (256, 384)), 1: ((0, 256), (256, 384)), 2: ((0, 128), (128, 256)), 3: ((0, 128), (128, 256))}
-        for j in range(LANES):
-            for t0, t1 in early[j]:
-                first_lookup(j, t0, t1)
-            for t0, t1 in early[j]:
-                second_lookup(j, t0, t1)
-        interleave(0)
-        for c, planes in ((1, (2, 3)), (2, (0, 1, 2, 3)), (3, (0, 1, 2, 3))):
-            t0, t1 = CHUNKS[c]
-            for j in planes:
-                first_lookup(j, t0, t1)
-            for j in planes:
-                second_lookup(j, t0, t1)
-            interleave(c)
-        for c in range(len(CHUNKS)):
-            quantise(c)
-
         for m in range(D // P):
-            acc = psum.tile([P, T], F32, name="acc%d" % m)
+            acc = psum.tile([P, T], F32, name="acc%d" % m, tag="bank%d" % m)
             nc.tensor.matmul_mx(
                 out=acc[:],
                 lhsT=w_codes[:, 2 * P * m : 2 * P * (m + 1)].bitcast(E2M1X4),
@@ -135,9 +133,41 @@ def tile_attend_gvq_r_x_kernel(tc, zT, cb, cb2, w_words, w_scales, offs, offs2, 
                 start=True,
                 stop=True,
             )
-            result = keep.tile([P, T], F32, name="result%d" % m)
-            if m % 2 == 0:
-                nc.scalar.copy(out=result[:], in_=acc[:])
-            else:
-                nc.vector.tensor_copy(out=result[:], in_=acc[:])
-            nc.sync.dma_start(out=out[P * m : P * (m + 1), :], in_=result[:])
+            result = keep.tile([P, MAIN], F32, name="result%d" % m)
+            nc.scalar.copy(out=result[:], in_=acc[:, 0:MAIN])
+            nc.sync.dma_start(out=out[P * m : P * (m + 1), 0:MAIN], in_=result[:])
+
+        free_part = keep.tile([P, 2, P], F32, name="free_part")
+        late = keep.tile([P, 6, P], F32, name="late", tag="stage")
+        last_part = [free_part[:, 0, :], free_part[:, 1, :], late[:, 4, :], late[:, 5, :]]
+        for j in range(LANES):
+            first_lookup(j, MAIN, T, last_part[j])
+        for j in range(LANES):
+            second_lookup(j, MAIN, T, last_part[j], late[:, j, :])
+        last_bf = keep.tile([P, P, LANES], BF16, name="last_bf", align_bytes=64)
+        last_codes = keep.tile([P, P], U32, name="last_codes", align_bytes=64)
+        last_exps = keep.tile([P, P], U8, name="last_exps", align_bytes=64)
+        nc.vector.tensor_scalar(out=woven(last_bf[:]), in0=by_lane(late[:, 0:LANES, :]), scalar1=-BETA, scalar2=None, op0=MULT)
+        nc.vector.quantize_mx(
+            out=last_codes[:].bitcast(E5M2X4),
+            scales=last_exps[:],
+            in_=last_bf[:].rearrange("p t j -> p (t j)"),
+        )
+        acc_t = psum.tile([P, D], F32, name="acc_t", tag="bank4")
+        nc.tensor.matmul_mx(
+            out=acc_t[:],
+            lhsT=last_codes[:].bitcast(E5M2X4),
+            lhsT_scale=last_exps[:],
+            rhs=w_codes[:].bitcast(E2M1X4),
+            rhs_scale=w_exps[:],
+            start=True,
+            stop=True,
+        )
+        for m in range(D // P):
+            rows = keep.tile([P, P], F32, name="rows%d" % m)
+            nc.scalar.copy(out=rows[:], in_=acc_t[:, P * m : P * (m + 1)])
+            turned = psum.tile([P, P], F32, name="turned%d" % m, tag="bank%d" % ((5 + m) % 8))
+            nc.tensor.transpose(turned[:], rows[:], identity[:])
+            piece = keep.tile([P, P], F32, name="piece%d" % m)
+            nc.vector.tensor_copy(out=piece[:], in_=turned[:])
+            nc.sync.dma_start(out=out[P * m : P * (m + 1), MAIN:T], in_=piece[:])

@@ -24,6 +24,9 @@ LANES = 4
 PER_COLUMN = 16
 MAIN = 384
 MULT = mybir.AluOpType.mult
+FIRST = 128
+LAST = T - MAIN
+WHOLE = ()
 
 
 def tile_attend_gvq_r_x_kernel(tc, zT, cb, cb2, w_words, w_scales, offs, offs2, out):
@@ -36,9 +39,11 @@ def tile_attend_gvq_r_x_kernel(tc, zT, cb, cb2, w_words, w_scales, offs, offs2, 
         keep = ctx.enter_context(tc.tile_pool(name="keep", bufs=1))
         psum = ctx.enter_context(tc.psum_pool(name="psum", bufs=1))
 
+        early_end = [T if j in WHOLE else MAIN for j in range(LANES)]
+        longest = [early_end[j] - (FIRST if j == 0 else 0) for j in range(LANES)]
         code = keep.tile([P, T // PER_COLUMN], U16, name="code")
         code2 = keep.tile([P, T // PER_COLUMN], U16, name="code2")
-        book = [keep.tile([P, C], F32, name="book%d" % j) for j in range(LANES)]
+        book = [keep.tile([P, 2 * longest[j]], F32, name="book%d" % j) for j in range(LANES)]
         book2 = [keep.tile([P, C], F32, name="book2_%d" % j) for j in range(LANES)]
         w_codes = keep.tile([P, 2 * D], U8, name="w_codes", align_bytes=64)
         w_exps = keep.tile([P, D], U8, name="w_exps", align_bytes=64)
@@ -57,27 +62,36 @@ def tile_attend_gvq_r_x_kernel(tc, zT, cb, cb2, w_words, w_scales, offs, offs2, 
             return piece[:, j - j0, t0 - a0 : t1 - a0]
 
         identity = keep.tile([P, P], F32, name="identity")
+        for j in range(LANES):
+            if 2 * longest[j] > C:
+                nc.gpsimd.memset(book[j][:, C:], 0.0)
         nc.gpsimd.memset(w_exps[:].bitcast(U32), 0)
         nc.gpsimd.memset(g_codes[:, MAIN:T], 0)
         nc.gpsimd.memset(g_exps[:, MAIN:T].bitcast(U32), 0)
         make_identity(nc, identity[:])
 
-        nc.sync.dma_start(out=book[0][:], in_=cb_planes[:, 0, :])
-        nc.sync.dma_start(code[:], offs)
-        load_z(nc.scalar, 0, 1, 0, 192)
-        load_z(nc.sync, 0, 1, 192, MAIN)
-        nc.sync.dma_start(out=book2[0][:], in_=cb2_planes[:, 0, :])
-        nc.sync.dma_start(code2[:], offs2)
-        nc.sync.dma_start(out=book[1][:], in_=cb_planes[:, 1, :])
-        load_z(nc.sync, 1, 2, 0, MAIN)
-        nc.sync.dma_start(out=book2[1][:], in_=cb2_planes[:, 1, :])
-        nc.sync.dma_start(out=book[2][:], in_=cb_planes[:, 2, :])
-        load_z(nc.sync, 2, 4, 0, 256)
-        nc.sync.dma_start(out=book[3][:], in_=cb_planes[:, 3, :])
-        for j in (2, 3):
+        def load_book(j):
+            nc.sync.dma_start(out=book[j][:, 0:C], in_=cb_planes[:, j, :])
+
+        def load_book2(j):
             nc.sync.dma_start(out=book2[j][:], in_=cb2_planes[:, j, :])
-        load_z(nc.sync, 2, 4, 256, MAIN)
-        load_z(nc.sync, 0, 4, MAIN, T)
+
+        load_book(0)
+        nc.sync.dma_start(code[:], offs)
+        load_z(nc.scalar, 0, 1, 0, FIRST)
+        load_z(nc.sync, 0, 1, FIRST, early_end[0])
+        load_book2(0)
+        nc.sync.dma_start(code2[:], offs2)
+        load_book(1)
+        load_z(nc.sync, 1, 2, 0, early_end[1])
+        load_book(2)
+        load_z(nc.sync, 2, 3, 0, early_end[2])
+        load_book2(1)
+        load_book(3)
+        load_z(nc.sync, 3, 4, 0, early_end[3])
+        load_book2(2)
+        load_book2(3)
+        load_z(nc.sync, len(WHOLE), LANES, MAIN, T)
         nc.sync.dma_start(out=w_codes[:].bitcast(I32), in_=w_words[0].bitcast(I32))
         for q in range(4):
             nc.sync.dma_start(
@@ -99,28 +113,32 @@ def tile_attend_gvq_r_x_kernel(tc, zT, cb, cb2, w_words, w_scales, offs, offs2, 
         def by_lane(neg):
             return neg.rearrange("p j (s i) -> p s j i", i=4)
 
-        part = [keep.tile([P, MAIN], F32, name="part%d" % j) for j in range(LANES)]
-        neg_e = keep.tile([P, LANES, MAIN], F32, name="neg_e", tag="stage")
-        for j in (0, 1):
-            for t0, t1 in ((0, 192), (192, MAIN)):
-                first_lookup(j, t0, t1, part[j][:, t0:t1])
-            for t0, t1 in ((0, 192), (192, MAIN)):
-                second_lookup(j, t0, t1, part[j][:, t0:t1], neg_e[:, j, t0:t1])
-        main_bf = []
-        for t0, t1 in ((0, 256), (256, MAIN)):
-            for j in (2, 3):
-                first_lookup(j, t0, t1, part[j][:, t0:t1])
-            for j in (2, 3):
-                second_lookup(j, t0, t1, part[j][:, t0:t1], neg_e[:, j, t0:t1])
-            g_bf = keep.tile([P, t1 - t0, LANES], BF16, name="g_bf%d" % t0, align_bytes=64)
-            nc.scalar.activation(out=woven(g_bf[:]), in_=by_lane(neg_e[:, :, t0:t1]), func=COPY, scale=-BETA)
-            main_bf.append((t0, t1, g_bf))
-        for t0, t1, g_bf in main_bf:
-            nc.vector.quantize_mx(
-                out=g_codes[:, t0:t1].bitcast(E5M2X4),
-                scales=g_exps[:, t0:t1],
-                in_=g_bf[:].rearrange("p t j -> p (t j)"),
-            )
+        def quantise(codes, exps, g_tile):
+            nc.vector.quantize_mx(out=codes.bitcast(E5M2X4), scales=exps, in_=g_tile.rearrange("p t j -> p (t j)"))
+
+        part = [keep.tile([P, early_end[j]], F32, name="part%d" % j) for j in range(LANES)]
+        steps = ((0, 256), (256, MAIN))
+        g_bf = [keep.tile([P, t1 - t0, LANES], BF16, name="g_bf%d" % t0, align_bytes=64) for t0, t1 in steps]
+        neg_low = keep.tile([P, 2, MAIN], F32, name="neg_low")
+        for t0, t1 in ((0, FIRST), (FIRST, early_end[0])):
+            first_lookup(0, t0, t1, part[0][:, t0:t1])
+        for t0, t1 in ((0, FIRST), (FIRST, MAIN)):
+            second_lookup(0, t0, t1, part[0][:, t0:t1], neg_low[:, 0, t0:t1])
+        for j in (1, 2):
+            first_lookup(j, 0, early_end[j], part[j][:])
+        second_lookup(1, 0, MAIN, part[1][:, 0:MAIN], neg_low[:, 1, :])
+        for k, (t0, t1) in enumerate(steps):
+            nc.scalar.activation(out=woven(g_bf[k][:, :, 0:2]), in_=by_lane(neg_low[:, :, t0:t1]), func=COPY, scale=-BETA)
+        first_lookup(3, 0, early_end[3], part[3][:])
+        neg_high = keep.tile([P, 2, MAIN], F32, name="neg_high", tag="stage")
+        second_lookup(2, 0, MAIN, part[2][:, 0:MAIN], neg_high[:, 0, :])
+        for t0 in range(0, MAIN, P):
+            second_lookup(3, t0, t0 + P, part[3][:, t0 : t0 + P], neg_high[:, 1, t0 : t0 + P])
+            k = t0 // 256
+            g_piece = g_bf[k][:, t0 - steps[k][0] : t0 - steps[k][0] + P, 2:4]
+            nc.scalar.activation(out=woven(g_piece), in_=by_lane(neg_high[:, :, t0 : t0 + P]), func=COPY, scale=-BETA)
+        for k, (t0, t1) in enumerate(steps):
+            quantise(g_codes[:, t0:t1], g_exps[:, t0:t1], g_bf[k][:])
 
         for m in range(D // P):
             acc = psum.tile([P, T], F32, name="acc%d" % m, tag="bank%d" % m)
@@ -139,20 +157,26 @@ def tile_attend_gvq_r_x_kernel(tc, zT, cb, cb2, w_words, w_scales, offs, offs2, 
 
         free_part = keep.tile([P, 2, P], F32, name="free_part")
         late = keep.tile([P, 6, P], F32, name="late", tag="stage")
-        last_part = [free_part[:, 0, :], free_part[:, 1, :], late[:, 4, :], late[:, 5, :]]
+        spare = [free_part[:, 0, :], free_part[:, 1, :], late[:, 4, :], late[:, 5, :]]
+        last_part = []
         for j in range(LANES):
-            first_lookup(j, MAIN, T, last_part[j])
-        for j in range(LANES):
+            if j in WHOLE:
+                last_part.append(part[j][:, MAIN:T])
+            else:
+                last_part.append(spare[j - len(WHOLE)])
+                first_lookup(j, MAIN, T, last_part[j])
+        for j in range(LANES - 1):
             second_lookup(j, MAIN, T, last_part[j], late[:, j, :])
-        last_bf = keep.tile([P, P, LANES], BF16, name="last_bf", align_bytes=64)
         last_codes = keep.tile([P, P], U32, name="last_codes", align_bytes=64)
         last_exps = keep.tile([P, P], U8, name="last_exps", align_bytes=64)
-        nc.vector.tensor_scalar(out=woven(last_bf[:]), in0=by_lane(late[:, 0:LANES, :]), scalar1=-BETA, scalar2=None, op0=MULT)
-        nc.vector.quantize_mx(
-            out=last_codes[:].bitcast(E5M2X4),
-            scales=last_exps[:],
-            in_=last_bf[:].rearrange("p t j -> p (t j)"),
-        )
+        halves = ((0, 64), (64, P))
+        for t0, t1 in halves:
+            second_lookup(3, MAIN + t0, MAIN + t1, last_part[3][:, t0:t1], late[:, 3, t0:t1])
+        last_bf = [keep.tile([P, t1 - t0, LANES], BF16, name="last_bf%d" % t0, align_bytes=64) for t0, t1 in halves]
+        for k, (t0, t1) in enumerate(halves):
+            nc.vector.tensor_scalar(out=woven(last_bf[k][:]), in0=by_lane(late[:, 0:LANES, t0:t1]), scalar1=-BETA, scalar2=None, op0=MULT)
+        for k, (t0, t1) in enumerate(halves):
+            quantise(last_codes[:, t0:t1], last_exps[:, t0:t1], last_bf[k][:])
         acc_t = psum.tile([P, D], F32, name="acc_t", tag="bank4")
         nc.tensor.matmul_mx(
             out=acc_t[:],
@@ -170,4 +194,4 @@ def tile_attend_gvq_r_x_kernel(tc, zT, cb, cb2, w_words, w_scales, offs, offs2, 
             nc.tensor.transpose(turned[:], rows[:], identity[:])
             piece = keep.tile([P, P], F32, name="piece%d" % m)
             nc.vector.tensor_copy(out=piece[:], in_=turned[:])
-            nc.sync.dma_start(out=out[P * m : P * (m + 1), MAIN:T], in_=piece[:])
+            (nc.sync, nc.scalar)[m % 2].dma_start(out=out[P * m : P * (m + 1), MAIN:T], in_=piece[:])

@@ -17,16 +17,15 @@ E5M2X4 = mybir.dt.float8_e5m2_x4
 E2M1X4 = mybir.dt.float4_e2m1fn_x4
 SUBTRACT = mybir.AluOpType.subtract
 ADD = mybir.AluOpType.add
+MULT = mybir.AluOpType.mult
 COPY = mybir.ActivationFunctionType.Copy
 
 P = 128
 LANES = 4
 PER_COLUMN = 16
 MAIN = 384
-MULT = mybir.AluOpType.mult
 FIRST = 128
-LAST = T - MAIN
-WHOLE = ()
+WHOLE = (0, 3)
 
 
 def tile_attend_gvq_r_x_kernel(tc, zT, cb, cb2, w_words, w_scales, offs, offs2, out):
@@ -41,14 +40,15 @@ def tile_attend_gvq_r_x_kernel(tc, zT, cb, cb2, w_words, w_scales, offs, offs2, 
 
         early_end = [T if j in WHOLE else MAIN for j in range(LANES)]
         longest = [early_end[j] - (FIRST if j == 0 else 0) for j in range(LANES)]
+        late_lanes = [j for j in range(LANES) if j not in WHOLE]
         code = keep.tile([P, T // PER_COLUMN], U16, name="code")
         code2 = keep.tile([P, T // PER_COLUMN], U16, name="code2")
         book = [keep.tile([P, 2 * longest[j]], F32, name="book%d" % j) for j in range(LANES)]
         book2 = [keep.tile([P, C], F32, name="book2_%d" % j) for j in range(LANES)]
         w_codes = keep.tile([P, 2 * D], U8, name="w_codes", align_bytes=64)
         w_exps = keep.tile([P, D], U8, name="w_exps", align_bytes=64)
-        g_codes = keep.tile([P, T], U32, name="g_codes", align_bytes=64)
-        g_exps = keep.tile([P, T], U8, name="g_exps", align_bytes=64)
+        g_codes = keep.tile([P, P + T], U32, name="g_codes", align_bytes=64)
+        g_exps = keep.tile([P, P + T], U8, name="g_exps", align_bytes=64)
 
         z_pieces = []
 
@@ -62,13 +62,10 @@ def tile_attend_gvq_r_x_kernel(tc, zT, cb, cb2, w_words, w_scales, offs, offs2, 
             return piece[:, j - j0, t0 - a0 : t1 - a0]
 
         identity = keep.tile([P, P], F32, name="identity")
-        for j in range(LANES):
-            if 2 * longest[j] > C:
-                nc.gpsimd.memset(book[j][:, C:], 0.0)
-        nc.gpsimd.memset(w_exps[:].bitcast(U32), 0)
-        nc.gpsimd.memset(g_codes[:, MAIN:T], 0)
-        nc.gpsimd.memset(g_exps[:, MAIN:T].bitcast(U32), 0)
         make_identity(nc, identity[:])
+        nc.gpsimd.memset(w_exps[:].bitcast(U32), 0)
+        nc.gpsimd.memset(g_codes[:, 0:P], 0)
+        nc.gpsimd.memset(g_exps[:, 0:P].bitcast(U32), 0)
 
         def load_book(j):
             nc.sync.dma_start(out=book[j][:, 0:C], in_=cb_planes[:, j, :])
@@ -80,10 +77,10 @@ def tile_attend_gvq_r_x_kernel(tc, zT, cb, cb2, w_words, w_scales, offs, offs2, 
         nc.sync.dma_start(code[:], offs)
         load_z(nc.scalar, 0, 1, 0, FIRST)
         load_z(nc.sync, 0, 1, FIRST, early_end[0])
-        load_book2(0)
-        nc.sync.dma_start(code2[:], offs2)
         load_book(1)
         load_z(nc.sync, 1, 2, 0, early_end[1])
+        load_book2(0)
+        nc.sync.dma_start(code2[:], offs2)
         load_book(2)
         load_z(nc.sync, 2, 3, 0, early_end[2])
         load_book2(1)
@@ -91,13 +88,16 @@ def tile_attend_gvq_r_x_kernel(tc, zT, cb, cb2, w_words, w_scales, offs, offs2, 
         load_z(nc.sync, 3, 4, 0, early_end[3])
         load_book2(2)
         load_book2(3)
-        load_z(nc.sync, len(WHOLE), LANES, MAIN, T)
+        load_z(nc.sync, late_lanes[0], late_lanes[-1] + 1, MAIN, T)
         nc.sync.dma_start(out=w_codes[:].bitcast(I32), in_=w_words[0].bitcast(I32))
         for q in range(4):
             nc.sync.dma_start(
                 out=w_exps[32 * q : 32 * q + 4, :].bitcast(I32),
                 in_=w_scales[0, 4 * q : 4 * q + 4, :].bitcast(I32),
             )
+        for j in range(LANES):
+            if 2 * longest[j] > C:
+                nc.gpsimd.memset(book[j][:, C:], 0.0)
 
         def first_lookup(j, t0, t1, part):
             window = book[j][:].indirect(code[:, t0 // PER_COLUMN : t1 // PER_COLUMN])
@@ -120,39 +120,43 @@ def tile_attend_gvq_r_x_kernel(tc, zT, cb, cb2, w_words, w_scales, offs, offs2, 
         steps = ((0, 256), (256, MAIN))
         g_bf = [keep.tile([P, t1 - t0, LANES], BF16, name="g_bf%d" % t0, align_bytes=64) for t0, t1 in steps]
         neg_low = keep.tile([P, 2, MAIN], F32, name="neg_low")
+        neg_high = keep.tile([P, 2, MAIN], F32, name="neg_high", tag="stage")
         for t0, t1 in ((0, FIRST), (FIRST, early_end[0])):
             first_lookup(0, t0, t1, part[0][:, t0:t1])
-        for t0, t1 in ((0, FIRST), (FIRST, MAIN)):
-            second_lookup(0, t0, t1, part[0][:, t0:t1], neg_low[:, 0, t0:t1])
-        for j in (1, 2):
-            first_lookup(j, 0, early_end[j], part[j][:])
+        first_lookup(1, 0, early_end[1], part[1][:])
+        second_lookup(0, 0, MAIN, part[0][:, 0:MAIN], neg_low[:, 0, :])
+        first_lookup(2, 0, early_end[2], part[2][:])
         second_lookup(1, 0, MAIN, part[1][:, 0:MAIN], neg_low[:, 1, :])
         for k, (t0, t1) in enumerate(steps):
             nc.scalar.activation(out=woven(g_bf[k][:, :, 0:2]), in_=by_lane(neg_low[:, :, t0:t1]), func=COPY, scale=-BETA)
         first_lookup(3, 0, early_end[3], part[3][:])
-        neg_high = keep.tile([P, 2, MAIN], F32, name="neg_high", tag="stage")
         second_lookup(2, 0, MAIN, part[2][:, 0:MAIN], neg_high[:, 0, :])
-        for t0 in range(0, MAIN, P):
-            second_lookup(3, t0, t0 + P, part[3][:, t0 : t0 + P], neg_high[:, 1, t0 : t0 + P])
+        for t0, t1 in ((0, P), (P, 256), (256, MAIN)):
+            second_lookup(3, t0, t1, part[3][:, t0:t1], neg_high[:, 1, t0:t1])
             k = t0 // 256
-            g_piece = g_bf[k][:, t0 - steps[k][0] : t0 - steps[k][0] + P, 2:4]
-            nc.scalar.activation(out=woven(g_piece), in_=by_lane(neg_high[:, :, t0 : t0 + P]), func=COPY, scale=-BETA)
+            g_piece = g_bf[k][:, t0 - steps[k][0] : t1 - steps[k][0], 2:4]
+            nc.scalar.activation(out=woven(g_piece), in_=by_lane(neg_high[:, :, t0:t1]), func=COPY, scale=-BETA)
+        shift = P
         for k, (t0, t1) in enumerate(steps):
-            quantise(g_codes[:, t0:t1], g_exps[:, t0:t1], g_bf[k][:])
+            quantise(g_codes[:, shift + t0 : shift + t1], g_exps[:, shift + t0 : shift + t1], g_bf[k][:])
 
-        for m in range(D // P):
-            acc = psum.tile([P, T], F32, name="acc%d" % m, tag="bank%d" % m)
+        def weights_pass(m, c0, bank):
+            acc = psum.tile([P, T], F32, name="acc%d" % m, tag="bank%d" % bank)
             nc.tensor.matmul_mx(
                 out=acc[:],
                 lhsT=w_codes[:, 2 * P * m : 2 * P * (m + 1)].bitcast(E2M1X4),
                 lhsT_scale=w_exps[:, P * m : P * (m + 1)],
-                rhs=g_codes[:].bitcast(E5M2X4),
-                rhs_scale=g_exps[:],
+                rhs=g_codes[:, c0 : c0 + T].bitcast(E5M2X4),
+                rhs_scale=g_exps[:, c0 : c0 + T],
                 start=True,
                 stop=True,
             )
+            return acc
+
+        for m in range(D // P - 1):
+            acc = weights_pass(m, 0, m)
             result = keep.tile([P, MAIN], F32, name="result%d" % m)
-            nc.scalar.copy(out=result[:], in_=acc[:, 0:MAIN])
+            nc.scalar.copy(out=result[:], in_=acc[:, shift : shift + MAIN])
             nc.sync.dma_start(out=out[P * m : P * (m + 1), 0:MAIN], in_=result[:])
 
         free_part = keep.tile([P, 2, P], F32, name="free_part")
@@ -163,12 +167,12 @@ def tile_attend_gvq_r_x_kernel(tc, zT, cb, cb2, w_words, w_scales, offs, offs2, 
             if j in WHOLE:
                 last_part.append(part[j][:, MAIN:T])
             else:
-                last_part.append(spare[j - len(WHOLE)])
+                last_part.append(spare[late_lanes.index(j)])
                 first_lookup(j, MAIN, T, last_part[j])
         for j in range(LANES - 1):
             second_lookup(j, MAIN, T, last_part[j], late[:, j, :])
-        last_codes = keep.tile([P, P], U32, name="last_codes", align_bytes=64)
-        last_exps = keep.tile([P, P], U8, name="last_exps", align_bytes=64)
+        last_codes = g_codes[:, T : T + P]
+        last_exps = g_exps[:, T : T + P]
         halves = ((0, 64), (64, P))
         for t0, t1 in halves:
             second_lookup(3, MAIN + t0, MAIN + t1, last_part[3][:, t0:t1], late[:, 3, t0:t1])
@@ -180,18 +184,29 @@ def tile_attend_gvq_r_x_kernel(tc, zT, cb, cb2, w_words, w_scales, offs, offs2, 
         acc_t = psum.tile([P, D], F32, name="acc_t", tag="bank4")
         nc.tensor.matmul_mx(
             out=acc_t[:],
-            lhsT=last_codes[:].bitcast(E5M2X4),
-            lhsT_scale=last_exps[:],
+            lhsT=last_codes[:, 0:P].bitcast(E5M2X4),
+            lhsT_scale=last_exps[:, 0:P],
             rhs=w_codes[:].bitcast(E2M1X4),
             rhs_scale=w_exps[:],
             start=True,
             stop=True,
         )
-        for m in range(D // P):
-            rows = keep.tile([P, P], F32, name="rows%d" % m)
-            nc.scalar.copy(out=rows[:], in_=acc_t[:, P * m : P * (m + 1)])
-            turned = psum.tile([P, P], F32, name="turned%d" % m, tag="bank%d" % ((5 + m) % 8))
-            nc.tensor.transpose(turned[:], rows[:], identity[:])
+        last = D // P - 1
+        acc = weights_pass(last, P, last)
+        rows = [keep.tile([P, P], F32, name="rows%d" % m) for m in range(last)]
+        for m in range(last):
+            nc.scalar.copy(out=rows[m][:], in_=acc_t[:, P * m : P * (m + 1)])
+        for t0, t1 in ((0, 256), (256, T)):
+            result = keep.tile([P, t1 - t0], F32, name="result%d_%d" % (last, t0))
+            nc.vector.tensor_copy(out=result[:], in_=acc[:, t0:t1])
+            nc.sync.dma_start(out=out[P * last : P * (last + 1), t0:t1], in_=result[:])
+        for m in range(last):
+            turned = psum.tile([P, P], F32, name="turned%d" % m, tag="bank%d" % (5 + m))
+            nc.tensor.transpose(turned[:], rows[m][:], identity[:])
             piece = keep.tile([P, P], F32, name="piece%d" % m)
-            nc.vector.tensor_copy(out=piece[:], in_=turned[:])
-            (nc.sync, nc.scalar)[m % 2].dma_start(out=out[P * m : P * (m + 1), MAIN:T], in_=piece[:])
+            if m < last - 1:
+                nc.scalar.copy(out=piece[:], in_=turned[:])
+                nc.sync.dma_start(out=out[P * m : P * (m + 1), MAIN:T], in_=piece[:])
+            else:
+                nc.vector.tensor_copy(out=piece[:], in_=turned[:])
+                nc.scalar.dma_start(out=out[P * m : P * (m + 1), MAIN:T], in_=piece[:])

@@ -25,7 +25,7 @@ LANES = 4
 PER_COLUMN = 16
 MAIN = 384
 FIRST = 128
-WHOLE = (0, 3)
+WHOLE = (0,)
 
 
 def tile_attend_gvq_r_x_kernel(tc, zT, cb, cb2, w_words, w_scales, offs, offs2, out):
@@ -159,9 +159,9 @@ def tile_attend_gvq_r_x_kernel(tc, zT, cb, cb2, w_words, w_scales, offs, offs2, 
             nc.scalar.copy(out=result[:], in_=acc[:, shift : shift + MAIN])
             nc.sync.dma_start(out=out[P * m : P * (m + 1), 0:MAIN], in_=result[:])
 
-        free_part = keep.tile([P, 2, P], F32, name="free_part")
-        late = keep.tile([P, 6, P], F32, name="late", tag="stage")
-        spare = [free_part[:, 0, :], free_part[:, 1, :], late[:, 4, :], late[:, 5, :]]
+        free_part = keep.tile([P, 3, P], F32, name="free_part")
+        late = keep.tile([P, LANES, P], F32, name="late", tag="stage")
+        spare = [free_part[:, k, :] for k in range(3)]
         last_part = []
         for j in range(LANES):
             if j in WHOLE:

@@ -117,10 +117,13 @@ def tile_attend_gvq_r_x_kernel(tc, zT, cb, cb2, w_words, w_scales, offs, offs2, 
             nc.vector.quantize_mx(out=codes.bitcast(E5M2X4), scales=exps, in_=g_tile.rearrange("p t j -> p (t j)"))
 
         part = [keep.tile([P, early_end[j]], F32, name="part%d" % j) for j in range(LANES)]
-        steps = ((0, 256), (256, MAIN))
-        g_bf = [keep.tile([P, t1 - t0, LANES], BF16, name="g_bf%d" % t0, align_bytes=64) for t0, t1 in steps]
+        steps = ((P, MAIN), (0, P))
         neg_low = keep.tile([P, 2, MAIN], F32, name="neg_low")
-        neg_high = keep.tile([P, 2, MAIN], F32, name="neg_high", tag="stage")
+        stage = keep.tile([P, 64 + 2 * P + 2 * MAIN], F32, name="stage", align_bytes=64)
+        neg_high = stage[:, 64 + 2 * P :].rearrange("p (j t) -> p j t", j=2)
+        late = stage[:, 0 : LANES * P].rearrange("p (j t) -> p j t", j=LANES)
+        g_wide = keep.tile([P, MAIN - P, LANES], BF16, name="g_wide", align_bytes=64)
+        g_bf = [g_wide[:], stage[:, 64 : 64 + 2 * P].bitcast(BF16).rearrange("p (t j) -> p t j", j=LANES)]
         for t0, t1 in ((0, FIRST), (FIRST, early_end[0])):
             first_lookup(0, t0, t1, part[0][:, t0:t1])
         first_lookup(1, 0, early_end[1], part[1][:])
@@ -131,14 +134,14 @@ def tile_attend_gvq_r_x_kernel(tc, zT, cb, cb2, w_words, w_scales, offs, offs2, 
             nc.scalar.activation(out=woven(g_bf[k][:, :, 0:2]), in_=by_lane(neg_low[:, :, t0:t1]), func=COPY, scale=-BETA)
         first_lookup(3, 0, early_end[3], part[3][:])
         second_lookup(2, 0, MAIN, part[2][:, 0:MAIN], neg_high[:, 0, :])
-        for t0, t1 in ((0, P), (P, 256), (256, MAIN)):
+        for t0, t1 in ((256, MAIN), (P, 256), (0, P)):
             second_lookup(3, t0, t1, part[3][:, t0:t1], neg_high[:, 1, t0:t1])
-            k = t0 // 256
+            k = 0 if t0 >= P else 1
             g_piece = g_bf[k][:, t0 - steps[k][0] : t1 - steps[k][0], 2:4]
             nc.scalar.activation(out=woven(g_piece), in_=by_lane(neg_high[:, :, t0:t1]), func=COPY, scale=-BETA)
         shift = P
         for k, (t0, t1) in enumerate(steps):
-            quantise(g_codes[:, shift + t0 : shift + t1], g_exps[:, shift + t0 : shift + t1], g_bf[k][:])
+            quantise(g_codes[:, shift + t0 : shift + t1], g_exps[:, shift + t0 : shift + t1], g_bf[k])
 
         def weights_pass(m, c0, bank):
             acc = psum.tile([P, T], F32, name="acc%d" % m, tag="bank%d" % bank)
@@ -159,28 +162,23 @@ def tile_attend_gvq_r_x_kernel(tc, zT, cb, cb2, w_words, w_scales, offs, offs2, 
             nc.scalar.copy(out=result[:], in_=acc[:, shift : shift + MAIN])
             nc.sync.dma_start(out=out[P * m : P * (m + 1), 0:MAIN], in_=result[:])
 
-        free_part = keep.tile([P, 3, P], F32, name="free_part")
-        late = keep.tile([P, LANES, P], F32, name="late", tag="stage")
-        spare = [free_part[:, k, :] for k in range(3)]
-        last_part = []
-        for j in range(LANES):
-            if j in WHOLE:
-                last_part.append(part[j][:, MAIN:T])
-            else:
-                last_part.append(spare[late_lanes.index(j)])
-                first_lookup(j, MAIN, T, last_part[j])
-        for j in range(LANES - 1):
+        free_part = keep.tile([P, LANES - 1, P], F32, name="free_part")
+        last_part = [part[0][:, MAIN:T]] + [free_part[:, j - 1, :] for j in range(1, LANES)]
+        for j in range(1, LANES):
+            first_lookup(j, MAIN, T, last_part[j])
+        second_lookup(0, MAIN, MAIN + 64, last_part[0][:, 0:64], late[:, 0, 0:64])
+        for j in (3, 2, 1):
             second_lookup(j, MAIN, T, last_part[j], late[:, j, :])
+        second_lookup(0, MAIN + 64, T, last_part[0][:, 64:P], late[:, 0, 64:P])
         last_codes = g_codes[:, T : T + P]
         last_exps = g_exps[:, T : T + P]
         halves = ((0, 64), (64, P))
+        last_bf = keep.tile([P, P, LANES], BF16, name="last_bf", align_bytes=64)
+        nc.vector.tensor_scalar(out=woven(last_bf[:, :, 2:4]), in0=by_lane(late[:, 2:4, :]), scalar1=-BETA, scalar2=None, op0=MULT)
         for t0, t1 in halves:
-            second_lookup(3, MAIN + t0, MAIN + t1, last_part[3][:, t0:t1], late[:, 3, t0:t1])
-        last_bf = [keep.tile([P, t1 - t0, LANES], BF16, name="last_bf%d" % t0, align_bytes=64) for t0, t1 in halves]
-        for k, (t0, t1) in enumerate(halves):
-            nc.vector.tensor_scalar(out=woven(last_bf[k][:]), in0=by_lane(late[:, 0:LANES, t0:t1]), scalar1=-BETA, scalar2=None, op0=MULT)
-        for k, (t0, t1) in enumerate(halves):
-            quantise(last_codes[:, t0:t1], last_exps[:, t0:t1], last_bf[k][:])
+            nc.vector.tensor_scalar(out=woven(last_bf[:, t0:t1, 0:2]), in0=by_lane(late[:, 0:2, t0:t1]), scalar1=-BETA, scalar2=None, op0=MULT)
+        for t0, t1 in halves:
+            quantise(last_codes[:, t0:t1], last_exps[:, t0:t1], last_bf[:, t0:t1, :])
         acc_t = psum.tile([P, D], F32, name="acc_t", tag="bank4")
         nc.tensor.matmul_mx(
             out=acc_t[:],

@@ -1,7 +1,6 @@
 from contextlib import ExitStack
 
 import concourse.mybir as mybir
-from concourse.masks import make_identity
 
 N_FEAT, T, C, D = 512, 512, 512, 512
 BETA = 0.25
@@ -15,7 +14,6 @@ U16 = mybir.dt.uint16
 U8 = mybir.dt.uint8
 E5M2X4 = mybir.dt.float8_e5m2_x4
 E2M1X4 = mybir.dt.float4_e2m1fn_x4
-SUBTRACT = mybir.AluOpType.subtract
 ADD = mybir.AluOpType.add
 MULT = mybir.AluOpType.mult
 COPY = mybir.ActivationFunctionType.Copy
@@ -23,9 +21,10 @@ COPY = mybir.ActivationFunctionType.Copy
 P = 128
 LANES = 4
 PER_COLUMN = 16
-MAIN = 384
-FIRST = 128
-WHOLE = (0,)
+HALF = T // 2
+CHUNK = 128
+CHUNKS = T // CHUNK
+BLOCKS = D // P
 
 
 def tile_attend_gvq_r_x_kernel(tc, zT, cb, cb2, w_words, w_scales, offs, offs2, out):
@@ -33,178 +32,101 @@ def tile_attend_gvq_r_x_kernel(tc, zT, cb, cb2, w_words, w_scales, offs, offs2, 
     z_planes = zT.rearrange("(p j) t -> p j t", j=LANES)
     cb_planes = cb.rearrange("(p j) c -> p j c", j=LANES)
     cb2_planes = cb2.rearrange("(p j) c -> p j c", j=LANES)
+    out_blocks = out.rearrange("(m p) t -> p m t", p=P)
 
     with ExitStack() as ctx:
         keep = ctx.enter_context(tc.tile_pool(name="keep", bufs=1))
         psum = ctx.enter_context(tc.psum_pool(name="psum", bufs=1))
 
-        early_end = [T if j in WHOLE else MAIN for j in range(LANES)]
-        longest = [early_end[j] - (FIRST if j == 0 else 0) for j in range(LANES)]
-        late_lanes = [j for j in range(LANES) if j not in WHOLE]
         code = keep.tile([P, T // PER_COLUMN], U16, name="code")
         code2 = keep.tile([P, T // PER_COLUMN], U16, name="code2")
-        book = [keep.tile([P, 2 * longest[j]], F32, name="book%d" % j) for j in range(LANES)]
+        book = [keep.tile([P, C], F32, name="book%d" % j) for j in range(LANES)]
         book2 = [keep.tile([P, C], F32, name="book2_%d" % j) for j in range(LANES)]
+        z = [keep.tile([P, LANES, HALF], F32, name="z%d" % h) for h in range(2)]
         w_codes = keep.tile([P, 2 * D], U8, name="w_codes", align_bytes=64)
         w_exps = keep.tile([P, D], U8, name="w_exps", align_bytes=64)
-        g_codes = keep.tile([P, P + T], U32, name="g_codes", align_bytes=64)
-        g_exps = keep.tile([P, P + T], U8, name="g_exps", align_bytes=64)
 
-        z_pieces = []
-
-        def load_z(queue, j0, j1, t0, t1):
-            piece = keep.tile([P, j1 - j0, t1 - t0], F32, name="z_%d_%d" % (j0, t0))
-            queue.dma_start(out=piece[:], in_=z_planes[:, j0:j1, t0:t1])
-            z_pieces.append((j0, j1, t0, t1, piece))
-
-        def z_of(j, t0, t1):
-            j0, a0, piece = [(j0, a0, piece) for j0, j1, a0, a1, piece in z_pieces if j0 <= j < j1 and a0 <= t0 and t1 <= a1][0]
-            return piece[:, j - j0, t0 - a0 : t1 - a0]
-
-        identity = keep.tile([P, P], F32, name="identity")
-        make_identity(nc, identity[:])
+        ones = keep.tile([P, 1], F32, name="ones")
+        neg_beta = keep.tile([P, 1], F32, name="neg_beta")
+        nc.gpsimd.memset(ones[:], 1.0)
+        nc.scalar.activation(out=neg_beta[:], in_=ones[:], func=COPY, scale=-BETA)
         nc.gpsimd.memset(w_exps[:].bitcast(U32), 0)
-        nc.gpsimd.memset(g_codes[:, 0:P], 0)
-        nc.gpsimd.memset(g_exps[:, 0:P].bitcast(U32), 0)
 
-        def load_book(j):
-            nc.sync.dma_start(out=book[j][:, 0:C], in_=cb_planes[:, j, :])
-
-        def load_book2(j):
+        for j in range(LANES):
             nc.sync.dma_start(out=book2[j][:], in_=cb2_planes[:, j, :])
-
-        load_book(0)
-        nc.sync.dma_start(code[:], offs)
-        load_z(nc.scalar, 0, 1, 0, FIRST)
-        load_z(nc.sync, 0, 1, FIRST, early_end[0])
-        load_book(1)
-        load_z(nc.sync, 1, 2, 0, early_end[1])
-        load_book2(0)
-        nc.sync.dma_start(code2[:], offs2)
-        load_book(2)
-        load_z(nc.sync, 2, 3, 0, early_end[2])
-        load_book2(1)
-        load_book(3)
-        load_z(nc.sync, 3, 4, 0, early_end[3])
-        load_book2(2)
-        load_book2(3)
-        load_z(nc.sync, late_lanes[0], late_lanes[-1] + 1, MAIN, T)
+            if j == 0:
+                nc.sync.dma_start(code2[:], offs2)
+            nc.sync.dma_start(out=book[j][:], in_=cb_planes[:, j, :])
+            if j == 0:
+                nc.sync.dma_start(code[:], offs)
+        nc.sync.dma_start(out=z[0][:], in_=z_planes[:, :, 0:HALF])
+        nc.sync.dma_start(out=z[1][:], in_=z_planes[:, :, HALF:T])
         nc.sync.dma_start(out=w_codes[:].bitcast(I32), in_=w_words[0].bitcast(I32))
         for q in range(4):
             nc.sync.dma_start(
                 out=w_exps[32 * q : 32 * q + 4, :].bitcast(I32),
                 in_=w_scales[0, 4 * q : 4 * q + 4, :].bitcast(I32),
             )
+
+        second = [keep.tile([P, LANES, HALF], F32, name="second%d" % h) for h in range(2)]
+        both = [keep.tile([P, LANES, HALF], F32, name="both%d" % h) for h in range(2)]
         for j in range(LANES):
-            if 2 * longest[j] > C:
-                nc.gpsimd.memset(book[j][:, C:], 0.0)
-
-        def first_lookup(j, t0, t1, part):
-            window = book[j][:].indirect(code[:, t0 // PER_COLUMN : t1 // PER_COLUMN])
-            nc.vector.tensor_tensor(part, window, z_of(j, t0, t1), SUBTRACT)
-
-        def second_lookup(j, t0, t1, part, neg):
-            window = book2[j][:].indirect(code2[:, t0 // PER_COLUMN : t1 // PER_COLUMN])
-            nc.vector.tensor_tensor(neg, window, part, ADD)
+            for h in range(2):
+                cols = slice(h * HALF // PER_COLUMN, (h + 1) * HALF // PER_COLUMN)
+                nc.scalar.activation(out=second[h][:, j, :], in_=book2[j][:].indirect(code2[:, cols]), func=COPY)
+                nc.vector.tensor_tensor(both[h][:, j, :], book[j][:].indirect(code[:, cols]), second[h][:, j, :], ADD)
 
         def woven(g_tile):
             return g_tile.rearrange("p (s i) j -> p s j i", i=4)
 
-        def by_lane(neg):
-            return neg.rearrange("p j (s i) -> p s j i", i=4)
+        def by_lane(e_tile):
+            return e_tile.rearrange("p j (s i) -> p s j i", i=4)
 
-        def quantise(codes, exps, g_tile):
-            nc.vector.quantize_mx(out=codes.bitcast(E5M2X4), scales=exps, in_=g_tile.rearrange("p t j -> p (t j)"))
+        scaled = [keep.tile([P, CHUNK, LANES], F32, name="scaled%d" % c) for c in range(CHUNKS)]
+        g_bf = [keep.tile([P, CHUNK, LANES], BF16, name="g_bf%d" % c, align_bytes=64) for c in range(CHUNKS)]
+        g_codes = [keep.tile([P, CHUNK], U32, name="g_codes%d" % c, align_bytes=64) for c in range(CHUNKS)]
+        g_exps = [keep.tile([P, CHUNK], U8, name="g_exps%d" % c, align_bytes=64) for c in range(CHUNKS)]
 
-        part = [keep.tile([P, early_end[j]], F32, name="part%d" % j) for j in range(LANES)]
-        steps = ((P, MAIN), (0, P))
-        neg_low = keep.tile([P, 2, MAIN], F32, name="neg_low")
-        stage = keep.tile([P, 64 + 2 * P + 2 * MAIN], F32, name="stage", align_bytes=64)
-        neg_high = stage[:, 64 + 2 * P :].rearrange("p (j t) -> p j t", j=2)
-        late = stage[:, 0 : LANES * P].rearrange("p (j t) -> p j t", j=LANES)
-        g_wide = keep.tile([P, MAIN - P, LANES], BF16, name="g_wide", align_bytes=64)
-        g_bf = [g_wide[:], stage[:, 64 : 64 + 2 * P].bitcast(BF16).rearrange("p (t j) -> p t j", j=LANES)]
-        for t0, t1 in ((0, FIRST), (FIRST, early_end[0])):
-            first_lookup(0, t0, t1, part[0][:, t0:t1])
-        first_lookup(1, 0, early_end[1], part[1][:])
-        second_lookup(0, 0, MAIN, part[0][:, 0:MAIN], neg_low[:, 0, :])
-        first_lookup(2, 0, early_end[2], part[2][:])
-        second_lookup(1, 0, MAIN, part[1][:, 0:MAIN], neg_low[:, 1, :])
-        for k, (t0, t1) in enumerate(steps):
-            nc.scalar.activation(out=woven(g_bf[k][:, :, 0:2]), in_=by_lane(neg_low[:, :, t0:t1]), func=COPY, scale=-BETA)
-        first_lookup(3, 0, early_end[3], part[3][:])
-        second_lookup(2, 0, MAIN, part[2][:, 0:MAIN], neg_high[:, 0, :])
-        for t0, t1 in ((256, MAIN), (P, 256), (0, P)):
-            second_lookup(3, t0, t1, part[3][:, t0:t1], neg_high[:, 1, t0:t1])
-            k = 0 if t0 >= P else 1
-            g_piece = g_bf[k][:, t0 - steps[k][0] : t1 - steps[k][0], 2:4]
-            nc.scalar.activation(out=woven(g_piece), in_=by_lane(neg_high[:, :, t0:t1]), func=COPY, scale=-BETA)
-        shift = P
-        for k, (t0, t1) in enumerate(steps):
-            quantise(g_codes[:, shift + t0 : shift + t1], g_exps[:, shift + t0 : shift + t1], g_bf[k])
+        def scale_codewords(c):
+            h, t0 = divmod(c * CHUNK, HALF)
+            nc.scalar.activation(out=woven(scaled[c][:]), in_=by_lane(both[h][:, :, t0 : t0 + CHUNK]), func=COPY, scale=neg_beta[:])
 
-        def weights_pass(m, c0, bank):
-            acc = psum.tile([P, T], F32, name="acc%d" % m, tag="bank%d" % bank)
-            nc.tensor.matmul_mx(
-                out=acc[:],
-                lhsT=w_codes[:, 2 * P * m : 2 * P * (m + 1)].bitcast(E2M1X4),
-                lhsT_scale=w_exps[:, P * m : P * (m + 1)],
-                rhs=g_codes[:, c0 : c0 + T].bitcast(E5M2X4),
-                rhs_scale=g_exps[:, c0 : c0 + T],
-                start=True,
-                stop=True,
-            )
+        def gradient(c):
+            h, t0 = divmod(c * CHUNK, HALF)
+            z_by_token = z[h][:, :, t0 : t0 + CHUNK].rearrange("p j t -> p t j")
+            nc.vector.scalar_tensor_tensor(out=g_bf[c][:], in0=z_by_token, scalar=BETA, in1=scaled[c][:], op0=MULT, op1=ADD)
+
+        def quantise(c):
+            nc.vector.quantize_mx(out=g_codes[c][:].bitcast(E5M2X4), scales=g_exps[c][:], in_=g_bf[c][:].rearrange("p t j -> p (t j)"))
+
+        def product(c, m0, m1, bank):
+            acc = psum.tile([P, m1 - m0, CHUNK], F32, name="acc%d_%d" % (c, m0), tag="bank%d" % bank)
+            for m in range(m0, m1):
+                nc.tensor.matmul_mx(
+                    out=acc[:, m - m0, :],
+                    lhsT=w_codes[:, 2 * P * m : 2 * P * (m + 1)].bitcast(E2M1X4),
+                    lhsT_scale=w_exps[:, P * m : P * (m + 1)],
+                    rhs=g_codes[c][:].bitcast(E5M2X4),
+                    rhs_scale=g_exps[c][:],
+                    start=True,
+                    stop=True,
+                )
             return acc
 
-        for m in range(D // P - 1):
-            acc = weights_pass(m, 0, m)
-            result = keep.tile([P, MAIN], F32, name="result%d" % m)
-            nc.scalar.copy(out=result[:], in_=acc[:, shift : shift + MAIN])
-            nc.sync.dma_start(out=out[P * m : P * (m + 1), 0:MAIN], in_=result[:])
+        def empty_and_store(c, m0, m1, acc, copy, queue):
+            result = keep.tile([P, m1 - m0, CHUNK], F32, name="result%d_%d" % (c, m0))
+            copy(out=result[:], in_=acc[:])
+            queue.dma_start(out=out_blocks[:, m0:m1, c * CHUNK : (c + 1) * CHUNK], in_=result[:])
 
-        free_part = keep.tile([P, LANES - 1, P], F32, name="free_part")
-        last_part = [part[0][:, MAIN:T]] + [free_part[:, j - 1, :] for j in range(1, LANES)]
-        for j in range(1, LANES):
-            first_lookup(j, MAIN, T, last_part[j])
-        second_lookup(0, MAIN, MAIN + 64, last_part[0][:, 0:64], late[:, 0, 0:64])
-        for j in (3, 2, 1):
-            second_lookup(j, MAIN, T, last_part[j], late[:, j, :])
-        second_lookup(0, MAIN + 64, T, last_part[0][:, 64:P], late[:, 0, 64:P])
-        last_codes = g_codes[:, T : T + P]
-        last_exps = g_exps[:, T : T + P]
-        halves = ((0, 64), (64, P))
-        last_bf = keep.tile([P, P, LANES], BF16, name="last_bf", align_bytes=64)
-        nc.vector.tensor_scalar(out=woven(last_bf[:, :, 2:4]), in0=by_lane(late[:, 2:4, :]), scalar1=-BETA, scalar2=None, op0=MULT)
-        for t0, t1 in halves:
-            nc.vector.tensor_scalar(out=woven(last_bf[:, t0:t1, 0:2]), in0=by_lane(late[:, 0:2, t0:t1]), scalar1=-BETA, scalar2=None, op0=MULT)
-        for t0, t1 in halves:
-            quantise(last_codes[:, t0:t1], last_exps[:, t0:t1], last_bf[:, t0:t1, :])
-        acc_t = psum.tile([P, D], F32, name="acc_t", tag="bank4")
-        nc.tensor.matmul_mx(
-            out=acc_t[:],
-            lhsT=last_codes[:, 0:P].bitcast(E5M2X4),
-            lhsT_scale=last_exps[:, 0:P],
-            rhs=w_codes[:].bitcast(E2M1X4),
-            rhs_scale=w_exps[:],
-            start=True,
-            stop=True,
-        )
-        last = D // P - 1
-        acc = weights_pass(last, P, last)
-        rows = [keep.tile([P, P], F32, name="rows%d" % m) for m in range(last)]
-        for m in range(last):
-            nc.scalar.copy(out=rows[m][:], in_=acc_t[:, P * m : P * (m + 1)])
-        for t0, t1 in ((0, 256), (256, T)):
-            result = keep.tile([P, t1 - t0], F32, name="result%d_%d" % (last, t0))
-            nc.vector.tensor_copy(out=result[:], in_=acc[:, t0:t1])
-            nc.sync.dma_start(out=out[P * last : P * (last + 1), t0:t1], in_=result[:])
-        for m in range(last):
-            turned = psum.tile([P, P], F32, name="turned%d" % m, tag="bank%d" % (5 + m))
-            nc.tensor.transpose(turned[:], rows[m][:], identity[:])
-            piece = keep.tile([P, P], F32, name="piece%d" % m)
-            if m < last - 1:
-                nc.scalar.copy(out=piece[:], in_=turned[:])
-                nc.sync.dma_start(out=out[P * m : P * (m + 1), MAIN:T], in_=piece[:])
-            else:
-                nc.vector.tensor_copy(out=piece[:], in_=turned[:])
-                nc.scalar.dma_start(out=out[P * m : P * (m + 1), MAIN:T], in_=piece[:])
+        last = CHUNKS - 1
+        for c in range(CHUNKS):
+            scale_codewords(c)
+        gradient(0)
+        for c in range(1, CHUNKS):
+            gradient(c)
+            quantise(c - 1)
+        for c in range(last):
+            empty_and_store(c, 0, BLOCKS, product(c, 0, BLOCKS, c), nc.scalar.copy, nc.sync)
+        quantise(last)
+        empty_and_store(last, 0, 2, product(last, 0, 2, last), nc.vector.tensor_copy, nc.sync)
+        empty_and_store(last, 2, BLOCKS, product(last, 2, BLOCKS, last + 1), nc.scalar.copy, nc.scalar)

@@ -60,21 +60,31 @@ def tile_attend_gvq_r_x_kernel(tc, zT, cb, cb2, w_words, w_scales, offs, offs2, 
             if j == 0:
                 nc.sync.dma_start(code[:], offs)
         nc.sync.dma_start(out=z[0][:], in_=z_planes[:, :, 0:HALF])
-        nc.sync.dma_start(out=z[1][:], in_=z_planes[:, :, HALF:T])
         nc.sync.dma_start(out=w_codes[:].bitcast(I32), in_=w_words[0].bitcast(I32))
+        nc.sync.dma_start(out=z[1][:], in_=z_planes[:, :, HALF:T])
         for q in range(4):
-            nc.sync.dma_start(
+            nc.gpsimd.dma_start(
                 out=w_exps[32 * q : 32 * q + 4, :].bitcast(I32),
                 in_=w_scales[0, 4 * q : 4 * q + 4, :].bitcast(I32),
             )
 
         second = [keep.tile([P, LANES, HALF], F32, name="second%d" % h) for h in range(2)]
         both = [keep.tile([P, LANES, HALF], F32, name="both%d" % h) for h in range(2)]
+
+        def look_up(j, t0, t1):
+            h, a0 = divmod(t0, HALF)
+            piece = slice(a0, a0 + t1 - t0)
+            cols = slice(t0 // PER_COLUMN, t1 // PER_COLUMN)
+            if j == 0 and h == 0:
+                nc.vector.tensor_copy(out=second[h][:, j, piece], in_=book2[j][:].indirect(code2[:, cols]))
+            else:
+                nc.scalar.activation(out=second[h][:, j, piece], in_=book2[j][:].indirect(code2[:, cols]), func=COPY)
+            nc.vector.tensor_tensor(both[h][:, j, piece], book[j][:].indirect(code[:, cols]), second[h][:, j, piece], ADD)
+
         for j in range(LANES):
-            for h in range(2):
-                cols = slice(h * HALF // PER_COLUMN, (h + 1) * HALF // PER_COLUMN)
-                nc.scalar.activation(out=second[h][:, j, :], in_=book2[j][:].indirect(code2[:, cols]), func=COPY)
-                nc.vector.tensor_tensor(both[h][:, j, :], book[j][:].indirect(code[:, cols]), second[h][:, j, :], ADD)
+            cuts = (0, CHUNK, HALF, T) if j in (0, LANES - 1) else (0, HALF, T)
+            for t0, t1 in zip(cuts, cuts[1:]):
+                look_up(j, t0, t1)
 
         def woven(g_tile):
             return g_tile.rearrange("p (s i) j -> p s j i", i=4)
@@ -83,7 +93,7 @@ def tile_attend_gvq_r_x_kernel(tc, zT, cb, cb2, w_words, w_scales, offs, offs2, 
             return e_tile.rearrange("p j (s i) -> p s j i", i=4)
 
         scaled = [keep.tile([P, CHUNK, LANES], F32, name="scaled%d" % c) for c in range(CHUNKS)]
-        g_bf = [keep.tile([P, CHUNK, LANES], BF16, name="g_bf%d" % c, align_bytes=64) for c in range(CHUNKS)]
+        g_bf = [keep.tile([P, CHUNK, LANES], BF16, name="g_bf%d" % c, tag="g_bf%d" % c, align_bytes=64) for c in range(CHUNKS)]
         g_codes = [keep.tile([P, CHUNK], U32, name="g_codes%d" % c, align_bytes=64) for c in range(CHUNKS)]
         g_exps = [keep.tile([P, CHUNK], U8, name="g_exps%d" % c, align_bytes=64) for c in range(CHUNKS)]
 
@@ -91,13 +101,13 @@ def tile_attend_gvq_r_x_kernel(tc, zT, cb, cb2, w_words, w_scales, offs, offs2, 
             h, t0 = divmod(c * CHUNK, HALF)
             nc.scalar.activation(out=woven(scaled[c][:]), in_=by_lane(both[h][:, :, t0 : t0 + CHUNK]), func=COPY, scale=neg_beta[:])
 
-        def gradient(c):
+        def gradient(c, a0=0, a1=CHUNK):
             h, t0 = divmod(c * CHUNK, HALF)
-            z_by_token = z[h][:, :, t0 : t0 + CHUNK].rearrange("p j t -> p t j")
-            nc.vector.scalar_tensor_tensor(out=g_bf[c][:], in0=z_by_token, scalar=BETA, in1=scaled[c][:], op0=MULT, op1=ADD)
+            z_by_token = z[h][:, :, t0 + a0 : t0 + a1].rearrange("p j t -> p t j")
+            nc.vector.scalar_tensor_tensor(out=g_bf[c][:, a0:a1, :], in0=z_by_token, scalar=BETA, in1=scaled[c][:, a0:a1, :], op0=MULT, op1=ADD)
 
-        def quantise(c):
-            nc.vector.quantize_mx(out=g_codes[c][:].bitcast(E5M2X4), scales=g_exps[c][:], in_=g_bf[c][:].rearrange("p t j -> p (t j)"))
+        def quantise(c, a0=0, a1=CHUNK):
+            nc.vector.quantize_mx(out=g_codes[c][:, a0:a1].bitcast(E5M2X4), scales=g_exps[c][:, a0:a1], in_=g_bf[c][:, a0:a1, :].rearrange("p t j -> p (t j)"))
 
         def product(c, m0, m1, bank):
             acc = psum.tile([P, m1 - m0, CHUNK], F32, name="acc%d_%d" % (c, m0), tag="bank%d" % bank)
@@ -114,7 +124,9 @@ def tile_attend_gvq_r_x_kernel(tc, zT, cb, cb2, w_words, w_scales, offs, offs2, 
             return acc
 
         def empty_and_store(c, m0, m1, acc, copy, queue):
-            result = keep.tile([P, m1 - m0, CHUNK], F32, name="result%d_%d" % (c, m0))
+            name = "result%d_%d" % (c, m0)
+            tag = "g_bf%d" % last if c == last - 1 and m0 == 0 else name
+            result = keep.tile([P, m1 - m0, CHUNK], F32, name=name, tag=tag, align_bytes=64)
             copy(out=result[:], in_=acc[:])
             queue.dma_start(out=out_blocks[:, m0:m1, c * CHUNK : (c + 1) * CHUNK], in_=result[:])
 
@@ -122,11 +134,15 @@ def tile_attend_gvq_r_x_kernel(tc, zT, cb, cb2, w_words, w_scales, offs, offs2, 
         for c in range(CHUNKS):
             scale_codewords(c)
         gradient(0)
-        for c in range(1, CHUNKS):
+        for c in range(1, last):
             gradient(c)
             quantise(c - 1)
-        for c in range(last):
-            empty_and_store(c, 0, BLOCKS, product(c, 0, BLOCKS, c), nc.scalar.copy, nc.sync)
-        quantise(last)
-        empty_and_store(last, 0, 2, product(last, 0, 2, last), nc.vector.tensor_copy, nc.sync)
-        empty_and_store(last, 2, BLOCKS, product(last, 2, BLOCKS, last + 1), nc.scalar.copy, nc.scalar)
+        gradient(last, 0, CHUNK // 2)
+        quantise(last - 1)
+        gradient(last, CHUNK // 2, CHUNK)
+        quantise(last, 0, CHUNK // 2)
+        quantise(last, CHUNK // 2, CHUNK)
+        for c in range(CHUNKS):
+            late = c >= last - 1
+            empty_and_store(c, 0, 2, product(c, 0, 2, 2 * c), nc.vector.tensor_copy if late else nc.scalar.copy, nc.sync)
+            empty_and_store(c, 2, BLOCKS, product(c, 2, BLOCKS, 2 * c + 1), nc.scalar.copy, nc.scalar if c == last else nc.sync)

@@ -32,7 +32,6 @@ def tile_attend_gvq_r_x_kernel(tc, zT, cb, cb2, w_words, w_scales, offs, offs2, 
     z_planes = zT.rearrange("(p j) t -> p j t", j=LANES)
     cb_planes = cb.rearrange("(p j) c -> p j c", j=LANES)
     cb2_planes = cb2.rearrange("(p j) c -> p j c", j=LANES)
-    out_blocks = out.rearrange("(m p) t -> p m t", p=P)
 
     with ExitStack() as ctx:
         keep = ctx.enter_context(tc.tile_pool(name="keep", bufs=1))
@@ -60,8 +59,8 @@ def tile_attend_gvq_r_x_kernel(tc, zT, cb, cb2, w_words, w_scales, offs, offs2, 
             if j == 0:
                 nc.sync.dma_start(code[:], offs)
         nc.sync.dma_start(out=z[0][:], in_=z_planes[:, :, 0:HALF])
-        nc.sync.dma_start(out=w_codes[:].bitcast(I32), in_=w_words[0].bitcast(I32))
         nc.sync.dma_start(out=z[1][:], in_=z_planes[:, :, HALF:T])
+        nc.sync.dma_start(out=w_codes[:].bitcast(I32), in_=w_words[0].bitcast(I32))
         for q in range(4):
             nc.gpsimd.dma_start(
                 out=w_exps[32 * q : 32 * q + 4, :].bitcast(I32),
@@ -93,9 +92,9 @@ def tile_attend_gvq_r_x_kernel(tc, zT, cb, cb2, w_words, w_scales, offs, offs2, 
             return e_tile.rearrange("p j (s i) -> p s j i", i=4)
 
         scaled = [keep.tile([P, CHUNK, LANES], F32, name="scaled%d" % c) for c in range(CHUNKS)]
-        g_bf = [keep.tile([P, CHUNK, LANES], BF16, name="g_bf%d" % c, tag="g_bf%d" % c, align_bytes=64) for c in range(CHUNKS)]
-        g_codes = [keep.tile([P, CHUNK], U32, name="g_codes%d" % c, align_bytes=64) for c in range(CHUNKS)]
-        g_exps = [keep.tile([P, CHUNK], U8, name="g_exps%d" % c, align_bytes=64) for c in range(CHUNKS)]
+        g_bf = {}
+        g_codes = [keep.tile([P, HALF], U32, name="g_codes%d" % h, align_bytes=64) for h in range(2)]
+        g_exps = [keep.tile([P, HALF], U8, name="g_exps%d" % h, align_bytes=64) for h in range(2)]
 
         def scale_codewords(c):
             h, t0 = divmod(c * CHUNK, HALF)
@@ -103,46 +102,52 @@ def tile_attend_gvq_r_x_kernel(tc, zT, cb, cb2, w_words, w_scales, offs, offs2, 
 
         def gradient(c, a0=0, a1=CHUNK):
             h, t0 = divmod(c * CHUNK, HALF)
+            if c not in g_bf:
+                g_bf[c] = keep.tile([P, CHUNK, LANES], BF16, name="g_bf%d" % c, tag="g_bf%d" % (c % 2), align_bytes=64)
             z_by_token = z[h][:, :, t0 + a0 : t0 + a1].rearrange("p j t -> p t j")
             nc.vector.scalar_tensor_tensor(out=g_bf[c][:, a0:a1, :], in0=z_by_token, scalar=BETA, in1=scaled[c][:, a0:a1, :], op0=MULT, op1=ADD)
 
         def quantise(c, a0=0, a1=CHUNK):
-            nc.vector.quantize_mx(out=g_codes[c][:, a0:a1].bitcast(E5M2X4), scales=g_exps[c][:, a0:a1], in_=g_bf[c][:, a0:a1, :].rearrange("p t j -> p (t j)"))
+            h, t0 = divmod(c * CHUNK, HALF)
+            cols = slice(t0 + a0, t0 + a1)
+            nc.vector.quantize_mx(out=g_codes[h][:, cols].bitcast(E5M2X4), scales=g_exps[h][:, cols], in_=g_bf[c][:, a0:a1, :].rearrange("p t j -> p (t j)"))
 
-        def product(c, m0, m1, bank):
-            acc = psum.tile([P, m1 - m0, CHUNK], F32, name="acc%d_%d" % (c, m0), tag="bank%d" % bank)
-            for m in range(m0, m1):
-                nc.tensor.matmul_mx(
-                    out=acc[:, m - m0, :],
-                    lhsT=w_codes[:, 2 * P * m : 2 * P * (m + 1)].bitcast(E2M1X4),
-                    lhsT_scale=w_exps[:, P * m : P * (m + 1)],
-                    rhs=g_codes[c][:].bitcast(E5M2X4),
-                    rhs_scale=g_exps[c][:],
-                    start=True,
-                    stop=True,
-                )
-            return acc
+        acc = [[psum.tile([P, HALF], F32, name="acc%d_%d" % (h, m)) for m in range(BLOCKS)] for h in range(2)]
 
-        def empty_and_store(c, m0, m1, acc, copy, queue):
-            name = "result%d_%d" % (c, m0)
-            tag = "g_bf%d" % last if c == last - 1 and m0 == 0 else name
-            result = keep.tile([P, m1 - m0, CHUNK], F32, name=name, tag=tag, align_bytes=64)
-            copy(out=result[:], in_=acc[:])
-            queue.dma_start(out=out_blocks[:, m0:m1, c * CHUNK : (c + 1) * CHUNK], in_=result[:])
+        def product(h, m, a0, a1):
+            nc.tensor.matmul_mx(
+                out=acc[h][m][:, a0:a1],
+                lhsT=w_codes[:, 2 * P * m : 2 * P * (m + 1)].bitcast(E2M1X4),
+                lhsT_scale=w_exps[:, P * m : P * (m + 1)],
+                rhs=g_codes[h][:, a0:a1].bitcast(E5M2X4),
+                rhs_scale=g_exps[h][:, a0:a1],
+                start=True,
+                stop=True,
+            )
+
+        def empty_and_store(h, m, copy):
+            result = keep.tile([P, HALF], F32, name="result%d_%d" % (h, m))
+            copy(out=result[:], in_=acc[h][m][:])
+            nc.sync.dma_start(out=out[P * m : P * (m + 1), h * HALF : (h + 1) * HALF], in_=result[:])
 
         last = CHUNKS - 1
         for c in range(CHUNKS):
             scale_codewords(c)
         gradient(0)
-        for c in range(1, last):
-            gradient(c)
-            quantise(c - 1)
+        gradient(1)
+        quantise(0)
+        quantise(1)
+        gradient(2)
         gradient(last, 0, CHUNK // 2)
-        quantise(last - 1)
+        quantise(2)
         gradient(last, CHUNK // 2, CHUNK)
         quantise(last, 0, CHUNK // 2)
         quantise(last, CHUNK // 2, CHUNK)
-        for c in range(CHUNKS):
-            late = c >= last - 1
-            empty_and_store(c, 0, 2, product(c, 0, 2, 2 * c), nc.vector.tensor_copy if late else nc.scalar.copy, nc.sync)
-            empty_and_store(c, 2, BLOCKS, product(c, 2, BLOCKS, 2 * c + 1), nc.scalar.copy, nc.scalar if c == last else nc.sync)
+        for m in range(BLOCKS):
+            product(0, m, 0, HALF)
+            empty_and_store(0, m, nc.scalar.copy)
+        for m in range(BLOCKS):
+            product(1, m, 0, CHUNK)
+        for m in range(BLOCKS):
+            product(1, m, CHUNK, HALF)
+            empty_and_store(1, m, nc.scalar.copy if m % 2 else nc.vector.tensor_copy)

@@ -32,6 +32,7 @@ def tile_attend_gvq_r_x_kernel(tc, zT, cb, cb2, w_words, w_scales, offs, offs2, 
     z_planes = zT.rearrange("(p j) t -> p j t", j=LANES)
     cb_planes = cb.rearrange("(p j) c -> p j c", j=LANES)
     cb2_planes = cb2.rearrange("(p j) c -> p j c", j=LANES)
+    out_blocks = out.rearrange("(m p) t -> p m t", p=P)
 
     with ExitStack() as ctx:
         keep = ctx.enter_context(tc.tile_pool(name="keep", bufs=1))
@@ -59,13 +60,13 @@ def tile_attend_gvq_r_x_kernel(tc, zT, cb, cb2, w_words, w_scales, offs, offs2, 
             if j == 0:
                 nc.sync.dma_start(code[:], offs)
         nc.sync.dma_start(out=z[0][:], in_=z_planes[:, :, 0:HALF])
-        nc.sync.dma_start(out=z[1][:], in_=z_planes[:, :, HALF:T])
-        nc.sync.dma_start(out=w_codes[:].bitcast(I32), in_=w_words[0].bitcast(I32))
         for q in range(4):
-            nc.gpsimd.dma_start(
+            nc.sync.dma_start(
                 out=w_exps[32 * q : 32 * q + 4, :].bitcast(I32),
                 in_=w_scales[0, 4 * q : 4 * q + 4, :].bitcast(I32),
             )
+        nc.sync.dma_start(out=z[1][:], in_=z_planes[:, :, HALF:T])
+        nc.sync.dma_start(out=w_codes[:].bitcast(I32), in_=w_words[0].bitcast(I32))
 
         second = [keep.tile([P, LANES, HALF], F32, name="second%d" % h) for h in range(2)]
         both = [keep.tile([P, LANES, HALF], F32, name="both%d" % h) for h in range(2)]
@@ -92,7 +93,8 @@ def tile_attend_gvq_r_x_kernel(tc, zT, cb, cb2, w_words, w_scales, offs, offs2, 
             return e_tile.rearrange("p j (s i) -> p s j i", i=4)
 
         scaled = [keep.tile([P, CHUNK, LANES], F32, name="scaled%d" % c) for c in range(CHUNKS)]
-        g_bf = {}
+        g_all = keep.tile([P, T - CHUNK // 2, LANES], BF16, name="g_all", align_bytes=64)
+        g_bf = [g_all[:, t0 : t0 + CHUNK, :] for t0 in (64, 192, 0, 320)]
         g_codes = [keep.tile([P, HALF], U32, name="g_codes%d" % h, align_bytes=64) for h in range(2)]
         g_exps = [keep.tile([P, HALF], U8, name="g_exps%d" % h, align_bytes=64) for h in range(2)]
 
@@ -102,8 +104,6 @@ def tile_attend_gvq_r_x_kernel(tc, zT, cb, cb2, w_words, w_scales, offs, offs2, 
 
         def gradient(c, a0=0, a1=CHUNK):
             h, t0 = divmod(c * CHUNK, HALF)
-            if c not in g_bf:
-                g_bf[c] = keep.tile([P, CHUNK, LANES], BF16, name="g_bf%d" % c, tag="g_bf%d" % (c % 2), align_bytes=64)
             z_by_token = z[h][:, :, t0 + a0 : t0 + a1].rearrange("p j t -> p t j")
             nc.vector.scalar_tensor_tensor(out=g_bf[c][:, a0:a1, :], in0=z_by_token, scalar=BETA, in1=scaled[c][:, a0:a1, :], op0=MULT, op1=ADD)
 
@@ -112,11 +112,9 @@ def tile_attend_gvq_r_x_kernel(tc, zT, cb, cb2, w_words, w_scales, offs, offs2, 
             cols = slice(t0 + a0, t0 + a1)
             nc.vector.quantize_mx(out=g_codes[h][:, cols].bitcast(E5M2X4), scales=g_exps[h][:, cols], in_=g_bf[c][:, a0:a1, :].rearrange("p t j -> p (t j)"))
 
-        acc = [[psum.tile([P, HALF], F32, name="acc%d_%d" % (h, m)) for m in range(BLOCKS)] for h in range(2)]
-
-        def product(h, m, a0, a1):
+        def product(acc, h, m, a0, a1):
             nc.tensor.matmul_mx(
-                out=acc[h][m][:, a0:a1],
+                out=acc,
                 lhsT=w_codes[:, 2 * P * m : 2 * P * (m + 1)].bitcast(E2M1X4),
                 lhsT_scale=w_exps[:, P * m : P * (m + 1)],
                 rhs=g_codes[h][:, a0:a1].bitcast(E5M2X4),
@@ -125,29 +123,39 @@ def tile_attend_gvq_r_x_kernel(tc, zT, cb, cb2, w_words, w_scales, offs, offs2, 
                 stop=True,
             )
 
-        def empty_and_store(h, m, copy):
-            result = keep.tile([P, HALF], F32, name="result%d_%d" % (h, m))
-            copy(out=result[:], in_=acc[h][m][:])
-            nc.sync.dma_start(out=out[P * m : P * (m + 1), h * HALF : (h + 1) * HALF], in_=result[:])
+        def empty_and_store(acc, m0, m1, t0, t1, copy):
+            result = keep.tile([P, m1 - m0, t1 - t0], F32, name="result%d_%d" % (m0, t0))
+            copy(out=result[:], in_=acc[:])
+            nc.sync.dma_start(out=out_blocks[:, m0:m1, t0:t1], in_=result[:])
 
         last = CHUNKS - 1
         for c in range(CHUNKS):
             scale_codewords(c)
         gradient(0)
         gradient(1)
+        gradient(2, 0, CHUNK // 2)
         quantise(0)
         quantise(1)
-        gradient(2)
+        gradient(2, CHUNK // 2, CHUNK)
         gradient(last, 0, CHUNK // 2)
         quantise(2)
         gradient(last, CHUNK // 2, CHUNK)
         quantise(last, 0, CHUNK // 2)
         quantise(last, CHUNK // 2, CHUNK)
         for m in range(BLOCKS):
-            product(0, m, 0, HALF)
-            empty_and_store(0, m, nc.scalar.copy)
-        for m in range(BLOCKS):
-            product(1, m, 0, CHUNK)
-        for m in range(BLOCKS):
-            product(1, m, CHUNK, HALF)
-            empty_and_store(1, m, nc.scalar.copy if m % 2 else nc.vector.tensor_copy)
+            acc = psum.tile([P, 1, HALF], F32, name="early%d" % m)
+            product(acc[:, 0, :], 0, m, 0, HALF)
+            empty_and_store(acc, m, m + 1, 0, HALF, nc.scalar.copy)
+        low = [psum.tile([P, 2, CHUNK], F32, name="low%d" % k) for k in range(2)]
+        high = [psum.tile([P, 1, HALF], F32, name="high%d" % k) for k in range(2)]
+        for m in range(2):
+            product(low[0][:, m, :], 1, m, 0, CHUNK)
+        empty_and_store(low[0], 0, 2, HALF, HALF + CHUNK, nc.scalar.copy)
+        for a0 in (0, CHUNK):
+            for k in range(2):
+                product(high[k][:, 0, a0 : a0 + CHUNK], 1, 2 + k, a0, a0 + CHUNK)
+        for m in range(2):
+            product(low[1][:, m, :], 1, m, CHUNK, HALF)
+        empty_and_store(high[0], 2, 3, HALF, T, nc.vector.tensor_copy)
+        empty_and_store(high[1], 3, 4, HALF, T, nc.scalar.copy)
+        empty_and_store(low[1], 0, 2, HALF + CHUNK, T, nc.vector.tensor_copy)

@@ -21,18 +21,22 @@ COPY = mybir.ActivationFunctionType.Copy
 P = 128
 LANES = 4
 PER_COLUMN = 16
+LINE = 4
 HALF = T // 2
 CHUNK = 128
 CHUNKS = T // CHUNK
-BLOCKS = D // P
+PAIR = 2
+QUADRANT = 32
 
 
 def tile_attend_gvq_r_x_kernel(tc, zT, cb, cb2, w_words, w_scales, offs, offs2, out):
     nc = tc.nc
-    z_planes = zT.rearrange("(p j) t -> p j t", j=LANES)
-    cb_planes = cb.rearrange("(p j) c -> p j c", j=LANES)
-    cb2_planes = cb2.rearrange("(p j) c -> p j c", j=LANES)
+    z_lanes = zT.rearrange("(p j) t -> p j t", j=LANES)
+    cb_lanes = cb.rearrange("(p j) c -> p j c", j=LANES)
+    cb2_lanes = cb2.rearrange("(p j) c -> p j c", j=LANES)
     out_blocks = out.rearrange("(m p) t -> p m t", p=P)
+    last_lane = LANES - 1
+    last_chunk = CHUNKS - 1
 
     with ExitStack() as ctx:
         keep = ctx.enter_context(tc.tile_pool(name="keep", bufs=1))
@@ -42,7 +46,9 @@ def tile_attend_gvq_r_x_kernel(tc, zT, cb, cb2, w_words, w_scales, offs, offs2, 
         code2 = keep.tile([P, T // PER_COLUMN], U16, name="code2")
         book = [keep.tile([P, C], F32, name="book%d" % j) for j in range(LANES)]
         book2 = [keep.tile([P, C], F32, name="book2_%d" % j) for j in range(LANES)]
-        z = [keep.tile([P, LANES, HALF], F32, name="z%d" % h) for h in range(2)]
+        z_early = keep.tile([P, LANES, HALF], F32, name="z_early")
+        z_late = [keep.tile([P, LANES, CHUNK], F32, name="z_late%d" % k) for k in range(2)]
+        z = [z_early[:, :, 0:CHUNK], z_early[:, :, CHUNK:HALF], z_late[0][:], z_late[1][:]]
         w_codes = keep.tile([P, 2 * D], U8, name="w_codes", align_bytes=64)
         w_exps = keep.tile([P, D], U8, name="w_exps", align_bytes=64)
 
@@ -52,73 +58,97 @@ def tile_attend_gvq_r_x_kernel(tc, zT, cb, cb2, w_words, w_scales, offs, offs2, 
         nc.scalar.activation(out=neg_beta[:], in_=ones[:], func=COPY, scale=-BETA)
         nc.gpsimd.memset(w_exps[:].bitcast(U32), 0)
 
+        nc.sync.dma_start(out=book2[0][:], in_=cb2_lanes[:, 0, :])
+        nc.sync.dma_start(code2[:], offs2)
         for j in range(LANES):
-            nc.sync.dma_start(out=book2[j][:], in_=cb2_planes[:, j, :])
-            if j == 0:
-                nc.sync.dma_start(code2[:], offs2)
-            nc.sync.dma_start(out=book[j][:], in_=cb_planes[:, j, :])
+            if j < last_lane:
+                nc.sync.dma_start(out=book2[j + 1][:], in_=cb2_lanes[:, j + 1, :])
+            nc.sync.dma_start(out=book[j][:], in_=cb_lanes[:, j, :])
             if j == 0:
                 nc.sync.dma_start(code[:], offs)
-        nc.sync.dma_start(out=z[0][:], in_=z_planes[:, :, 0:HALF])
-        for q in range(4):
+        nc.sync.dma_start(out=z_early[:], in_=z_lanes[:, :, 0:HALF])
+        nc.sync.dma_start(out=w_codes[:].bitcast(I32), in_=w_words[0].bitcast(I32))
+        for q in range(P // QUADRANT):
             nc.sync.dma_start(
-                out=w_exps[32 * q : 32 * q + 4, :].bitcast(I32),
+                out=w_exps[QUADRANT * q : QUADRANT * q + 4, :].bitcast(I32),
                 in_=w_scales[0, 4 * q : 4 * q + 4, :].bitcast(I32),
             )
-        nc.sync.dma_start(out=z[1][:], in_=z_planes[:, :, HALF:T])
-        nc.sync.dma_start(out=w_codes[:].bitcast(I32), in_=w_words[0].bitcast(I32))
+        for k in range(2):
+            nc.sync.dma_start(out=z_late[k][:], in_=z_lanes[:, :, HALF + k * CHUNK : HALF + (k + 1) * CHUNK])
 
-        second = [keep.tile([P, LANES, HALF], F32, name="second%d" % h) for h in range(2)]
         both = [keep.tile([P, LANES, HALF], F32, name="both%d" % h) for h in range(2)]
+        second = {}
 
-        def look_up(j, t0, t1):
-            h, a0 = divmod(t0, HALF)
-            piece = slice(a0, a0 + t1 - t0)
-            cols = slice(t0 // PER_COLUMN, t1 // PER_COLUMN)
-            if j == 0 and h == 0:
-                nc.vector.tensor_copy(out=second[h][:, j, piece], in_=book2[j][:].indirect(code2[:, cols]))
+        def entries(codes, t0, t1):
+            return codes[:, t0 // PER_COLUMN : t1 // PER_COLUMN]
+
+        def look_up_second(j, t0, t1, place=None):
+            if place is None:
+                place = keep.tile([P, t1 - t0], F32, name="second%d_%d" % (j, t0))[:]
+            second[j, t0] = place
+            window = book2[j][:].indirect(entries(code2, t0, t1))
+            if j == 0:
+                nc.vector.tensor_copy(out=place, in_=window)
             else:
-                nc.scalar.activation(out=second[h][:, j, piece], in_=book2[j][:].indirect(code2[:, cols]), func=COPY)
-            nc.vector.tensor_tensor(both[h][:, j, piece], book[j][:].indirect(code[:, cols]), second[h][:, j, piece], ADD)
+                nc.scalar.activation(out=place, in_=window, func=COPY)
 
-        for j in range(LANES):
-            cuts = (0, CHUNK, HALF, T) if j in (0, LANES - 1) else (0, HALF, T)
-            for t0, t1 in zip(cuts, cuts[1:]):
-                look_up(j, t0, t1)
+        def look_up_first(j, t0, t1):
+            h, a0 = divmod(t0, HALF)
+            window = book[j][:].indirect(entries(code, t0, t1))
+            nc.vector.tensor_tensor(both[h][:, j, a0 : a0 + t1 - t0], window, second[j, t0], ADD)
 
-        def woven(g_tile):
-            return g_tile.rearrange("p (s i) j -> p s j i", i=4)
-
-        def by_lane(e_tile):
-            return e_tile.rearrange("p j (s i) -> p s j i", i=4)
+        for j in range(last_lane):
+            for t0 in (0, HALF):
+                look_up_second(j, t0, t0 + HALF)
+        look_up_second(last_lane, 0, CHUNK, both[1][:, last_lane - 1, 0:CHUNK])
+        look_up_second(last_lane, CHUNK, HALF)
+        look_up_second(last_lane, HALF, T)
+        for j in range(last_lane - 1):
+            for t0 in (0, HALF):
+                look_up_first(j, t0, t0 + HALF)
+        look_up_first(last_lane - 1, 0, HALF)
+        look_up_first(last_lane, 0, CHUNK)
+        look_up_first(last_lane, CHUNK, HALF)
+        look_up_first(last_lane - 1, HALF, T)
+        first_late = keep.tile([P, HALF], F32, name="first_late")
+        nc.scalar.activation(out=first_late[:], in_=book[last_lane][:].indirect(entries(code, HALF, T)), func=COPY)
+        nc.vector.tensor_tensor(both[1][:, last_lane, :], first_late[:], second[last_lane, HALF], ADD)
 
         scaled = [keep.tile([P, CHUNK, LANES], F32, name="scaled%d" % c) for c in range(CHUNKS)]
-        g_all = keep.tile([P, T - CHUNK // 2, LANES], BF16, name="g_all", align_bytes=64)
-        g_bf = [g_all[:, t0 : t0 + CHUNK, :] for t0 in (64, 192, 0, 320)]
+        g_bf = [keep.tile([P, CHUNK, LANES], BF16, name="g_bf%d" % c, align_bytes=64) for c in range(CHUNKS)]
         g_codes = [keep.tile([P, HALF], U32, name="g_codes%d" % h, align_bytes=64) for h in range(2)]
         g_exps = [keep.tile([P, HALF], U8, name="g_exps%d" % h, align_bytes=64) for h in range(2)]
 
         def scale_codewords(c):
             h, t0 = divmod(c * CHUNK, HALF)
-            nc.scalar.activation(out=woven(scaled[c][:]), in_=by_lane(both[h][:, :, t0 : t0 + CHUNK]), func=COPY, scale=neg_beta[:])
+            nc.scalar.activation(
+                out=scaled[c][:].rearrange("p (s i) j -> p s j i", i=LINE),
+                in_=both[h][:, :, t0 : t0 + CHUNK].rearrange("p j (s i) -> p s j i", i=LINE),
+                func=COPY,
+                scale=neg_beta[:],
+            )
 
-        def gradient(c, a0=0, a1=CHUNK):
-            h, t0 = divmod(c * CHUNK, HALF)
-            z_by_token = z[h][:, :, t0 + a0 : t0 + a1].rearrange("p j t -> p t j")
+        def gradient(c, a0, a1):
+            z_by_token = z[c][:, :, a0:a1].rearrange("p j t -> p t j")
             nc.vector.scalar_tensor_tensor(out=g_bf[c][:, a0:a1, :], in0=z_by_token, scalar=BETA, in1=scaled[c][:, a0:a1, :], op0=MULT, op1=ADD)
 
-        def quantise(c, a0=0, a1=CHUNK):
+        def quantise(c, a0, a1):
             h, t0 = divmod(c * CHUNK, HALF)
             cols = slice(t0 + a0, t0 + a1)
-            nc.vector.quantize_mx(out=g_codes[h][:, cols].bitcast(E5M2X4), scales=g_exps[h][:, cols], in_=g_bf[c][:, a0:a1, :].rearrange("p t j -> p (t j)"))
+            nc.vector.quantize_mx(
+                out=g_codes[h][:, cols].bitcast(E5M2X4),
+                scales=g_exps[h][:, cols],
+                in_=g_bf[c][:, a0:a1, :].rearrange("p t j -> p (t j)"),
+            )
 
-        def product(acc, h, m, a0, a1):
+        def product(acc, m, c):
+            h, t0 = divmod(c * CHUNK, HALF)
             nc.tensor.matmul_mx(
                 out=acc,
                 lhsT=w_codes[:, 2 * P * m : 2 * P * (m + 1)].bitcast(E2M1X4),
                 lhsT_scale=w_exps[:, P * m : P * (m + 1)],
-                rhs=g_codes[h][:, a0:a1].bitcast(E5M2X4),
-                rhs_scale=g_exps[h][:, a0:a1],
+                rhs=g_codes[h][:, t0 : t0 + CHUNK].bitcast(E5M2X4),
+                rhs_scale=g_exps[h][:, t0 : t0 + CHUNK],
                 start=True,
                 stop=True,
             )
@@ -128,34 +158,33 @@ def tile_attend_gvq_r_x_kernel(tc, zT, cb, cb2, w_words, w_scales, offs, offs2, 
             copy(out=result[:], in_=acc[:])
             nc.sync.dma_start(out=out_blocks[:, m0:m1, t0:t1], in_=result[:])
 
-        last = CHUNKS - 1
         for c in range(CHUNKS):
             scale_codewords(c)
-        gradient(0)
-        gradient(1)
-        gradient(2, 0, CHUNK // 2)
-        quantise(0)
-        quantise(1)
-        gradient(2, CHUNK // 2, CHUNK)
-        gradient(last, 0, CHUNK // 2)
-        quantise(2)
-        gradient(last, CHUNK // 2, CHUNK)
-        quantise(last, 0, CHUNK // 2)
-        quantise(last, CHUNK // 2, CHUNK)
-        for m in range(BLOCKS):
-            acc = psum.tile([P, 1, HALF], F32, name="early%d" % m)
-            product(acc[:, 0, :], 0, m, 0, HALF)
-            empty_and_store(acc, m, m + 1, 0, HALF, nc.scalar.copy)
-        low = [psum.tile([P, 2, CHUNK], F32, name="low%d" % k) for k in range(2)]
-        high = [psum.tile([P, 1, HALF], F32, name="high%d" % k) for k in range(2)]
-        for m in range(2):
-            product(low[0][:, m, :], 1, m, 0, CHUNK)
-        empty_and_store(low[0], 0, 2, HALF, HALF + CHUNK, nc.scalar.copy)
-        for a0 in (0, CHUNK):
-            for k in range(2):
-                product(high[k][:, 0, a0 : a0 + CHUNK], 1, 2 + k, a0, a0 + CHUNK)
-        for m in range(2):
-            product(low[1][:, m, :], 1, m, CHUNK, HALF)
-        empty_and_store(high[0], 2, 3, HALF, T, nc.vector.tensor_copy)
-        empty_and_store(high[1], 3, 4, HALF, T, nc.scalar.copy)
-        empty_and_store(low[1], 0, 2, HALF + CHUNK, T, nc.vector.tensor_copy)
+        middle = CHUNK // 2
+        gradient(0, 0, CHUNK)
+        for c in range(1, CHUNKS):
+            gradient(c, 0, middle)
+            quantise(c - 1, 0, CHUNK)
+            gradient(c, middle, CHUNK)
+        quantise(last_chunk, 0, middle)
+        quantise(last_chunk, middle, CHUNK)
+
+        for c in range(2):
+            for m0 in (0, PAIR):
+                acc = psum.tile([P, PAIR, CHUNK], F32, name="early%d_%d" % (c, m0))
+                for m in range(PAIR):
+                    product(acc[:, m, :], m0 + m, c)
+                empty_and_store(acc, m0, m0 + PAIR, c * CHUNK, (c + 1) * CHUNK, nc.scalar.copy)
+        low = [psum.tile([P, PAIR, CHUNK], F32, name="low%d" % k) for k in range(2)]
+        high = [psum.tile([P, 1, HALF], F32, name="high%d" % k) for k in range(PAIR)]
+        for m in range(PAIR):
+            product(low[0][:, m, :], m, last_chunk - 1)
+        empty_and_store(low[0], 0, PAIR, HALF, HALF + CHUNK, nc.scalar.copy)
+        for k in range(2):
+            for m in range(PAIR):
+                product(high[m][:, 0, k * CHUNK : (k + 1) * CHUNK], PAIR + m, last_chunk - 1 + k)
+        for m in range(PAIR):
+            product(low[1][:, m, :], m, last_chunk)
+        empty_and_store(high[0], PAIR, PAIR + 1, HALF, T, nc.vector.tensor_copy)
+        empty_and_store(high[1], PAIR + 1, PAIR + 2, HALF, T, nc.scalar.copy)
+        empty_and_store(low[1], 0, PAIR, HALF + CHUNK, T, nc.vector.tensor_copy)

@@ -21,7 +21,6 @@ COPY = mybir.ActivationFunctionType.Copy
 P = 128
 LANES = 4
 PER_COLUMN = 16
-LINE = 4
 HALF = T // 2
 CHUNK = 128
 CHUNKS = T // CHUNK
@@ -35,8 +34,6 @@ def tile_attend_gvq_r_x_kernel(tc, zT, cb, cb2, w_words, w_scales, offs, offs2, 
     cb_lanes = cb.rearrange("(p j) c -> p j c", j=LANES)
     cb2_lanes = cb2.rearrange("(p j) c -> p j c", j=LANES)
     out_blocks = out.rearrange("(m p) t -> p m t", p=P)
-    last_lane = LANES - 1
-    last_chunk = CHUNKS - 1
 
     with ExitStack() as ctx:
         keep = ctx.enter_context(tc.tile_pool(name="keep", bufs=1))
@@ -46,9 +43,7 @@ def tile_attend_gvq_r_x_kernel(tc, zT, cb, cb2, w_words, w_scales, offs, offs2, 
         code2 = keep.tile([P, T // PER_COLUMN], U16, name="code2")
         book = [keep.tile([P, C], F32, name="book%d" % j) for j in range(LANES)]
         book2 = [keep.tile([P, C], F32, name="book2_%d" % j) for j in range(LANES)]
-        z_early = keep.tile([P, LANES, HALF], F32, name="z_early")
-        z_late = [keep.tile([P, LANES, CHUNK], F32, name="z_late%d" % k) for k in range(2)]
-        z = [z_early[:, :, 0:CHUNK], z_early[:, :, CHUNK:HALF], z_late[0][:], z_late[1][:]]
+        z = [keep.tile([P, LANES, CHUNK], F32, name="z%d" % c) for c in range(CHUNKS)]
         w_codes = keep.tile([P, 2 * D], U8, name="w_codes", align_bytes=64)
         w_exps = keep.tile([P, D], U8, name="w_exps", align_bytes=64)
 
@@ -60,131 +55,119 @@ def tile_attend_gvq_r_x_kernel(tc, zT, cb, cb2, w_words, w_scales, offs, offs2, 
 
         nc.sync.dma_start(out=book2[0][:], in_=cb2_lanes[:, 0, :])
         nc.sync.dma_start(code2[:], offs2)
-        for j in range(LANES):
-            if j < last_lane:
-                nc.sync.dma_start(out=book2[j + 1][:], in_=cb2_lanes[:, j + 1, :])
+        nc.sync.dma_start(out=book[0][:], in_=cb_lanes[:, 0, :])
+        nc.sync.dma_start(code[:], offs)
+        for j in range(1, LANES):
+            nc.sync.dma_start(out=book2[j][:], in_=cb2_lanes[:, j, :])
             nc.sync.dma_start(out=book[j][:], in_=cb_lanes[:, j, :])
-            if j == 0:
-                nc.sync.dma_start(code[:], offs)
-        nc.sync.dma_start(out=z_early[:], in_=z_lanes[:, :, 0:HALF])
+        nc.sync.dma_start(out=z[0][:], in_=z_lanes[:, :, 0:CHUNK])
         nc.sync.dma_start(out=w_codes[:].bitcast(I32), in_=w_words[0].bitcast(I32))
         for q in range(P // QUADRANT):
             nc.sync.dma_start(
                 out=w_exps[QUADRANT * q : QUADRANT * q + 4, :].bitcast(I32),
                 in_=w_scales[0, 4 * q : 4 * q + 4, :].bitcast(I32),
             )
-        for k in range(2):
-            nc.sync.dma_start(out=z_late[k][:], in_=z_lanes[:, :, HALF + k * CHUNK : HALF + (k + 1) * CHUNK])
+        for c in range(1, CHUNKS):
+            nc.sync.dma_start(out=z[c][:], in_=z_lanes[:, :, c * CHUNK : (c + 1) * CHUNK])
 
+        second = [[keep.tile([P, HALF], F32, name="second%d_%d" % (j, h)) for h in range(2)] for j in range(LANES)]
         both = [keep.tile([P, LANES, HALF], F32, name="both%d" % h) for h in range(2)]
-        second = {}
+        scaled = [keep.tile([P, LANES, HALF], F32, name="scaled%d" % h) for h in range(2)]
 
         def entries(codes, t0, t1):
             return codes[:, t0 // PER_COLUMN : t1 // PER_COLUMN]
 
-        def look_up_second(j, t0, t1, place=None):
-            if place is None:
-                place = keep.tile([P, t1 - t0], F32, name="second%d_%d" % (j, t0))[:]
-            second[j, t0] = place
-            window = book2[j][:].indirect(entries(code2, t0, t1))
-            if j == 0:
-                nc.vector.tensor_copy(out=place, in_=window)
-            else:
-                nc.scalar.activation(out=place, in_=window, func=COPY)
-
         def look_up_first(j, t0, t1):
             h, a0 = divmod(t0, HALF)
             window = book[j][:].indirect(entries(code, t0, t1))
-            nc.vector.tensor_tensor(both[h][:, j, a0 : a0 + t1 - t0], window, second[j, t0], ADD)
+            nc.vector.tensor_tensor(both[h][:, j, a0 : a0 + t1 - t0], window, second[j][h][:, a0 : a0 + t1 - t0], ADD)
 
-        for j in range(last_lane):
-            for t0 in (0, HALF):
-                look_up_second(j, t0, t0 + HALF)
-        look_up_second(last_lane, 0, CHUNK, both[1][:, last_lane - 1, 0:CHUNK])
-        look_up_second(last_lane, CHUNK, HALF)
-        look_up_second(last_lane, HALF, T)
-        for j in range(last_lane - 1):
-            for t0 in (0, HALF):
-                look_up_first(j, t0, t0 + HALF)
-        look_up_first(last_lane - 1, 0, HALF)
-        look_up_first(last_lane, 0, CHUNK)
-        look_up_first(last_lane, CHUNK, HALF)
-        look_up_first(last_lane - 1, HALF, T)
         first_late = keep.tile([P, HALF], F32, name="first_late")
-        nc.scalar.activation(out=first_late[:], in_=book[last_lane][:].indirect(entries(code, HALF, T)), func=COPY)
-        nc.vector.tensor_tensor(both[1][:, last_lane, :], first_late[:], second[last_lane, HALF], ADD)
+        nc.vector.tensor_copy(out=second[0][0][:], in_=book2[0][:].indirect(entries(code2, 0, HALF)))
+        nc.scalar.activation(out=second[0][1][:], in_=book2[0][:].indirect(entries(code2, HALF, T)), func=COPY, scale=-BETA)
+        nc.scalar.activation(out=first_late[:], in_=book[0][:].indirect(entries(code, HALF, T)), func=COPY, scale=-BETA)
+        look_up_first(0, 0, HALF)
+        nc.vector.tensor_tensor(scaled[1][:, 0, :], first_late[:], second[0][1][:], ADD)
+        nc.vector.tensor_scalar(out=scaled[0][:, 0, :], in0=both[0][:, 0, :], scalar1=-BETA, scalar2=None, op0=MULT)
+        for j in range(1, LANES):
+            for h in range(2):
+                nc.scalar.activation(out=second[j][h][:], in_=book2[j][:].indirect(entries(code2, h * HALF, (h + 1) * HALF)), func=COPY)
+            if j < LANES - 1:
+                for h in range(2):
+                    look_up_first(j, h * HALF, (h + 1) * HALF)
 
-        scaled = [keep.tile([P, CHUNK, LANES], F32, name="scaled%d" % c) for c in range(CHUNKS)]
         g_bf = [keep.tile([P, CHUNK, LANES], BF16, name="g_bf%d" % c, align_bytes=64) for c in range(CHUNKS)]
-        g_codes = [keep.tile([P, HALF], U32, name="g_codes%d" % h, align_bytes=64) for h in range(2)]
-        g_exps = [keep.tile([P, HALF], U8, name="g_exps%d" % h, align_bytes=64) for h in range(2)]
+        g_codes = [keep.tile([P, CHUNK], U32, name="g_codes%d" % c, align_bytes=64) for c in range(CHUNKS)]
+        g_exps = [keep.tile([P, CHUNK], U8, name="g_exps%d" % c, align_bytes=64) for c in range(CHUNKS)]
 
         def scale_codewords(c):
             h, t0 = divmod(c * CHUNK, HALF)
-            nc.scalar.activation(
-                out=scaled[c][:].rearrange("p (s i) j -> p s j i", i=LINE),
-                in_=both[h][:, :, t0 : t0 + CHUNK].rearrange("p j (s i) -> p s j i", i=LINE),
-                func=COPY,
-                scale=neg_beta[:],
-            )
+            nc.scalar.activation(out=scaled[h][:, 1:LANES, t0 : t0 + CHUNK], in_=both[h][:, 1:LANES, t0 : t0 + CHUNK], func=COPY, scale=neg_beta[:])
 
         def gradient(c, a0, a1):
-            z_by_token = z[c][:, :, a0:a1].rearrange("p j t -> p t j")
-            nc.vector.scalar_tensor_tensor(out=g_bf[c][:, a0:a1, :], in0=z_by_token, scalar=BETA, in1=scaled[c][:, a0:a1, :], op0=MULT, op1=ADD)
+            h, t0 = divmod(c * CHUNK, HALF)
+            nc.vector.scalar_tensor_tensor(
+                out=g_bf[c][:, a0:a1, :],
+                in0=z[c][:, :, a0:a1].rearrange("p j t -> p t j"),
+                scalar=BETA,
+                in1=scaled[h][:, :, t0 + a0 : t0 + a1].rearrange("p j t -> p t j"),
+                op0=MULT,
+                op1=ADD,
+            )
 
         def quantise(c, a0, a1):
-            h, t0 = divmod(c * CHUNK, HALF)
-            cols = slice(t0 + a0, t0 + a1)
             nc.vector.quantize_mx(
-                out=g_codes[h][:, cols].bitcast(E5M2X4),
-                scales=g_exps[h][:, cols],
+                out=g_codes[c][:, a0:a1].bitcast(E5M2X4),
+                scales=g_exps[c][:, a0:a1],
                 in_=g_bf[c][:, a0:a1, :].rearrange("p t j -> p (t j)"),
             )
 
         def product(acc, m, c):
-            h, t0 = divmod(c * CHUNK, HALF)
             nc.tensor.matmul_mx(
                 out=acc,
                 lhsT=w_codes[:, 2 * P * m : 2 * P * (m + 1)].bitcast(E2M1X4),
                 lhsT_scale=w_exps[:, P * m : P * (m + 1)],
-                rhs=g_codes[h][:, t0 : t0 + CHUNK].bitcast(E5M2X4),
-                rhs_scale=g_exps[h][:, t0 : t0 + CHUNK],
+                rhs=g_codes[c][:].bitcast(E5M2X4),
+                rhs_scale=g_exps[c][:],
                 start=True,
                 stop=True,
             )
 
-        def empty_and_store(acc, m0, m1, t0, t1, copy):
-            result = keep.tile([P, m1 - m0, t1 - t0], F32, name="result%d_%d" % (m0, t0))
-            copy(out=result[:], in_=acc[:])
-            nc.sync.dma_start(out=out_blocks[:, m0:m1, t0:t1], in_=result[:])
-
-        for c in range(CHUNKS):
-            scale_codewords(c)
+        last = LANES - 1
         middle = CHUNK // 2
+        for c in range(CHUNKS - 1):
+            look_up_first(last, c * CHUNK, (c + 1) * CHUNK)
+            scale_codewords(c)
         gradient(0, 0, CHUNK)
-        for c in range(1, CHUNKS):
+        look_up_first(last, T - CHUNK, T)
+        scale_codewords(CHUNKS - 1)
+        quantise(0, 0, CHUNK)
+        gradient(1, 0, CHUNK)
+        for c in range(2, CHUNKS):
             gradient(c, 0, middle)
             quantise(c - 1, 0, CHUNK)
             gradient(c, middle, CHUNK)
-        quantise(last_chunk, 0, middle)
-        quantise(last_chunk, middle, CHUNK)
+        quantise(CHUNKS - 1, 0, middle)
+        quantise(CHUNKS - 1, middle, CHUNK)
 
-        for c in range(2):
+        for c in range(CHUNKS - 1):
+            result = keep.tile([P, LANES, CHUNK], F32, name="result%d" % c)
             for m0 in (0, PAIR):
-                acc = psum.tile([P, PAIR, CHUNK], F32, name="early%d_%d" % (c, m0))
+                acc = psum.tile([P, PAIR, CHUNK], F32, name="acc%d_%d" % (c, m0))
                 for m in range(PAIR):
                     product(acc[:, m, :], m0 + m, c)
-                empty_and_store(acc, m0, m0 + PAIR, c * CHUNK, (c + 1) * CHUNK, nc.scalar.copy)
-        low = [psum.tile([P, PAIR, CHUNK], F32, name="low%d" % k) for k in range(2)]
-        high = [psum.tile([P, 1, HALF], F32, name="high%d" % k) for k in range(PAIR)]
-        for m in range(PAIR):
-            product(low[0][:, m, :], m, last_chunk - 1)
-        empty_and_store(low[0], 0, PAIR, HALF, HALF + CHUNK, nc.scalar.copy)
-        for k in range(2):
+                nc.scalar.copy(out=result[:, m0 : m0 + PAIR, :], in_=acc[:])
+                if c == 0:
+                    nc.sync.dma_start(out=out_blocks[:, m0 : m0 + PAIR, 0:CHUNK], in_=result[:, m0 : m0 + PAIR, :])
+            if c > 0:
+                nc.sync.dma_start(out=out_blocks[:, :, c * CHUNK : (c + 1) * CHUNK], in_=result[:])
+        c = CHUNKS - 1
+        names = ["acc3_0", "acc3_2", "acc0_0", "acc0_2"]
+        for m0 in (0, PAIR):
+            result = keep.tile([P, PAIR, CHUNK], F32, name="result3_%d" % m0)
             for m in range(PAIR):
-                product(high[m][:, 0, k * CHUNK : (k + 1) * CHUNK], PAIR + m, last_chunk - 1 + k)
-        for m in range(PAIR):
-            product(low[1][:, m, :], m, last_chunk)
-        empty_and_store(high[0], PAIR, PAIR + 1, HALF, T, nc.vector.tensor_copy)
-        empty_and_store(high[1], PAIR + 1, PAIR + 2, HALF, T, nc.scalar.copy)
-        empty_and_store(low[1], 0, PAIR, HALF + CHUNK, T, nc.vector.tensor_copy)
+                acc = psum.tile([P, CHUNK], F32, name=names[m0 + m])
+                product(acc[:], m0 + m, c)
+                copy = nc.vector.tensor_copy if m == 0 else nc.scalar.copy
+                copy(out=result[:, m, :], in_=acc[:])
+            nc.sync.dma_start(out=out_blocks[:, m0 : m0 + PAIR, c * CHUNK : T], in_=result[:])

@@ -157,10 +157,7 @@ def tile_attend_gvq_r_x_kernel(tc, zT, cb, cb2, w_words, w_scales, offs, offs2, 
                 for m in range(PAIR):
                     product(acc[:, m, :], m0 + m, c)
                 nc.scalar.copy(out=result[:, m0 : m0 + PAIR, :], in_=acc[:])
-                if c == 0:
-                    nc.sync.dma_start(out=out_blocks[:, m0 : m0 + PAIR, 0:CHUNK], in_=result[:, m0 : m0 + PAIR, :])
-            if c > 0:
-                nc.sync.dma_start(out=out_blocks[:, :, c * CHUNK : (c + 1) * CHUNK], in_=result[:])
+                nc.sync.dma_start(out=out_blocks[:, m0 : m0 + PAIR, c * CHUNK : (c + 1) * CHUNK], in_=result[:, m0 : m0 + PAIR, :])
         c = CHUNKS - 1
         names = ["acc3_0", "acc3_2", "acc0_0", "acc0_2"]
         for m0 in (0, PAIR):

@@ -34,6 +34,8 @@ def tile_attend_gvq_r_x_kernel(tc, zT, cb, cb2, w_words, w_scales, offs, offs2, 
     cb_lanes = cb.rearrange("(p j) c -> p j c", j=LANES)
     cb2_lanes = cb2.rearrange("(p j) c -> p j c", j=LANES)
     out_blocks = out.rearrange("(m p) t -> p m t", p=P)
+    last = LANES - 1
+    middle = CHUNK // 2
 
     with ExitStack() as ctx:
         keep = ctx.enter_context(tc.tile_pool(name="keep", bufs=1))
@@ -43,7 +45,7 @@ def tile_attend_gvq_r_x_kernel(tc, zT, cb, cb2, w_words, w_scales, offs, offs2, 
         code2 = keep.tile([P, T // PER_COLUMN], U16, name="code2")
         book = [keep.tile([P, C], F32, name="book%d" % j) for j in range(LANES)]
         book2 = [keep.tile([P, C], F32, name="book2_%d" % j) for j in range(LANES)]
-        z = [keep.tile([P, LANES, CHUNK], F32, name="z%d" % c) for c in range(CHUNKS)]
+        z = [keep.tile([P, LANES, CHUNK], F32, name="z%d" % c)[:] for c in range(CHUNKS)]
         w_codes = keep.tile([P, 2 * D], U8, name="w_codes", align_bytes=64)
         w_exps = keep.tile([P, D], U8, name="w_exps", align_bytes=64)
 
@@ -60,49 +62,70 @@ def tile_attend_gvq_r_x_kernel(tc, zT, cb, cb2, w_words, w_scales, offs, offs2, 
         for j in range(1, LANES):
             nc.sync.dma_start(out=book2[j][:], in_=cb2_lanes[:, j, :])
             nc.sync.dma_start(out=book[j][:], in_=cb_lanes[:, j, :])
-        nc.sync.dma_start(out=z[0][:], in_=z_lanes[:, :, 0:CHUNK])
-        nc.sync.dma_start(out=w_codes[:].bitcast(I32), in_=w_words[0].bitcast(I32))
-        for q in range(P // QUADRANT):
-            nc.sync.dma_start(
-                out=w_exps[QUADRANT * q : QUADRANT * q + 4, :].bitcast(I32),
-                in_=w_scales[0, 4 * q : 4 * q + 4, :].bitcast(I32),
-            )
-        for c in range(1, CHUNKS):
-            nc.sync.dma_start(out=z[c][:], in_=z_lanes[:, :, c * CHUNK : (c + 1) * CHUNK])
+        for c in range(CHUNKS):
+            nc.sync.dma_start(out=z[c], in_=z_lanes[:, :, c * CHUNK : (c + 1) * CHUNK])
+            if c == 0:
+                nc.sync.dma_start(out=w_codes[:].bitcast(I32), in_=w_words[0].bitcast(I32))
+                for q in range(P // QUADRANT):
+                    nc.sync.dma_start(
+                        out=w_exps[QUADRANT * q : QUADRANT * q + 4, :].bitcast(I32),
+                        in_=w_scales[0, 4 * q : 4 * q + 4, :].bitcast(I32),
+                    )
 
-        second = [[keep.tile([P, HALF], F32, name="second%d_%d" % (j, h)) for h in range(2)] for j in range(LANES)]
-        both = [keep.tile([P, LANES, HALF], F32, name="both%d" % h) for h in range(2)]
-        scaled = [keep.tile([P, LANES, HALF], F32, name="scaled%d" % h) for h in range(2)]
+        both = keep.tile([P, LANES, T], F32, name="both")
+        scaled_all = keep.tile([P, LANES, T], F32, name="scaled")
+        scaled = [scaled_all[:, :, 0:HALF], scaled_all[:, :, HALF:T]]
+        second = [[keep.tile([P, HALF], F32, name="second%d_%d" % (j, h))[:] if (j, h) != (2, 0) else None for h in range(2)] for j in range(last)]
+        second[2][0] = scaled_all[:, 1, 0:HALF]
+        late = keep.tile([P, CHUNK], F32, name="late")[:]
+        second_last = [late, scaled_all[:, 2, T - CHUNK : T]] + [keep.tile([P, CHUNK], F32, name="second3_c%d" % c)[:] for c in (2, 3)]
+        first_late = keep.tile([P, HALF], F32, name="first_late")[:]
 
         def entries(codes, t0, t1):
             return codes[:, t0 // PER_COLUMN : t1 // PER_COLUMN]
 
-        def look_up_first(j, t0, t1):
+        def on_vector(j, t0, t1):
             h, a0 = divmod(t0, HALF)
-            window = book[j][:].indirect(entries(code, t0, t1))
-            nc.vector.tensor_tensor(both[h][:, j, a0 : a0 + t1 - t0], window, second[j][h][:, a0 : a0 + t1 - t0], ADD)
+            other = second_last[t0 // CHUNK] if j == last else second[j][h][:, a0 : a0 + t1 - t0]
+            nc.vector.tensor_tensor(both[:, j, t0:t1], book[j][:].indirect(entries(code, t0, t1)), other, ADD)
 
-        first_late = keep.tile([P, HALF], F32, name="first_late")
-        nc.vector.tensor_copy(out=second[0][0][:], in_=book2[0][:].indirect(entries(code2, 0, HALF)))
-        nc.scalar.activation(out=second[0][1][:], in_=book2[0][:].indirect(entries(code2, HALF, T)), func=COPY, scale=-BETA)
-        nc.scalar.activation(out=first_late[:], in_=book[0][:].indirect(entries(code, HALF, T)), func=COPY, scale=-BETA)
-        look_up_first(0, 0, HALF)
-        nc.vector.tensor_tensor(scaled[1][:, 0, :], first_late[:], second[0][1][:], ADD)
-        nc.vector.tensor_scalar(out=scaled[0][:, 0, :], in0=both[0][:, 0, :], scalar1=-BETA, scalar2=None, op0=MULT)
-        for j in range(1, LANES):
+        def on_scalar(place, window, codes, t0, t1, factor):
+            nc.scalar.activation(out=place, in_=window[:].indirect(entries(codes, t0, t1)), func=COPY, scale=factor)
+
+        def scale_on_scalar(j0, j1, t0, t1):
+            nc.scalar.activation(out=scaled_all[:, j0:j1, t0:t1], in_=both[:, j0:j1, t0:t1], func=COPY, scale=neg_beta[:])
+
+        def scale_on_vector(j, t0, t1):
+            nc.vector.tensor_scalar(out=scaled_all[:, j, t0:t1], in0=both[:, j, t0:t1], scalar1=-BETA, scalar2=None, op0=MULT)
+
+        def add_late(j, values):
+            nc.vector.tensor_tensor(scaled[1][:, j, :], values, second[j][1], ADD)
+
+        nc.vector.tensor_copy(out=second[0][0], in_=book2[0][:].indirect(entries(code2, 0, HALF)))
+        on_scalar(second[0][1], book2[0], code2, HALF, T, -BETA)
+        on_scalar(first_late, book[0], code, HALF, T, -BETA)
+        on_vector(0, 0, HALF)
+        add_late(0, first_late)
+        scale_on_vector(0, 0, HALF)
+        for j in (1, 2):
             for h in range(2):
-                nc.scalar.activation(out=second[j][h][:], in_=book2[j][:].indirect(entries(code2, h * HALF, (h + 1) * HALF)), func=COPY)
-            if j < LANES - 1:
-                for h in range(2):
-                    look_up_first(j, h * HALF, (h + 1) * HALF)
+                on_scalar(second[j][h], book2[j], code2, h * HALF, (h + 1) * HALF, 1.0)
+            for h in range(2):
+                on_vector(j, h * HALF, (h + 1) * HALF)
+        scale_on_vector(1, 0, T)
+        for c in range(CHUNKS):
+            on_scalar(second_last[c], book2[last], code2, c * CHUNK, (c + 1) * CHUNK, 1.0 if c < CHUNKS - 1 else -BETA)
+        for c in range(CHUNKS - 1):
+            on_vector(last, c * CHUNK, (c + 1) * CHUNK)
+        scale_on_scalar(2, LANES, 0, CHUNK)
+        on_scalar(late, book[last], code, T - CHUNK, T, -BETA)
+        scale_on_scalar(2, LANES, CHUNK, HALF)
+        scale_on_scalar(2, LANES, HALF, HALF + CHUNK)
+        scale_on_scalar(2, last, T - CHUNK, T)
 
-        g_bf = [keep.tile([P, CHUNK, LANES], BF16, name="g_bf%d" % c, align_bytes=64) for c in range(CHUNKS)]
+        g_bf = [keep.tile([P, CHUNK, LANES], BF16, name="g_bf%d" % c, align_bytes=64)[:] for c in range(CHUNKS)]
         g_codes = [keep.tile([P, CHUNK], U32, name="g_codes%d" % c, align_bytes=64) for c in range(CHUNKS)]
         g_exps = [keep.tile([P, CHUNK], U8, name="g_exps%d" % c, align_bytes=64) for c in range(CHUNKS)]
-
-        def scale_codewords(c):
-            h, t0 = divmod(c * CHUNK, HALF)
-            nc.scalar.activation(out=scaled[h][:, 1:LANES, t0 : t0 + CHUNK], in_=both[h][:, 1:LANES, t0 : t0 + CHUNK], func=COPY, scale=neg_beta[:])
 
         def gradient(c, a0, a1):
             h, t0 = divmod(c * CHUNK, HALF)
@@ -133,31 +156,25 @@ def tile_attend_gvq_r_x_kernel(tc, zT, cb, cb2, w_words, w_scales, offs, offs2, 
                 stop=True,
             )
 
-        last = LANES - 1
-        middle = CHUNK // 2
-        for c in range(CHUNKS - 1):
-            look_up_first(last, c * CHUNK, (c + 1) * CHUNK)
-            scale_codewords(c)
         gradient(0, 0, CHUNK)
-        look_up_first(last, T - CHUNK, T)
-        scale_codewords(CHUNKS - 1)
+        nc.vector.tensor_tensor(scaled_all[:, last, T - CHUNK : T], late, second_last[CHUNKS - 1], ADD)
         quantise(0, 0, CHUNK)
         gradient(1, 0, CHUNK)
         for c in range(2, CHUNKS):
             gradient(c, 0, middle)
             quantise(c - 1, 0, CHUNK)
             gradient(c, middle, CHUNK)
-        quantise(CHUNKS - 1, 0, middle)
-        quantise(CHUNKS - 1, middle, CHUNK)
+        quantise(3, 0, middle)
+        quantise(3, middle, CHUNK)
 
         for c in range(CHUNKS - 1):
-            result = keep.tile([P, LANES, CHUNK], F32, name="result%d" % c)
             for m0 in (0, PAIR):
                 acc = psum.tile([P, PAIR, CHUNK], F32, name="acc%d_%d" % (c, m0))
                 for m in range(PAIR):
                     product(acc[:, m, :], m0 + m, c)
-                nc.scalar.copy(out=result[:, m0 : m0 + PAIR, :], in_=acc[:])
-                nc.sync.dma_start(out=out_blocks[:, m0 : m0 + PAIR, c * CHUNK : (c + 1) * CHUNK], in_=result[:, m0 : m0 + PAIR, :])
+                result = keep.tile([P, PAIR, CHUNK], F32, name="result%d_%d" % (c, m0))[:]
+                nc.scalar.copy(out=result, in_=acc[:])
+                nc.sync.dma_start(out=out_blocks[:, m0 : m0 + PAIR, c * CHUNK : (c + 1) * CHUNK], in_=result)
         c = CHUNKS - 1
         names = ["acc3_0", "acc3_2", "acc0_0", "acc0_2"]
         for m0 in (0, PAIR):

@@ -67,7 +67,7 @@ def tile_attend_gvq_r_x_kernel(tc, zT, cb, cb2, w_words, w_scales, offs, offs2, 
             if c == 0:
                 nc.sync.dma_start(out=w_codes[:].bitcast(I32), in_=w_words[0].bitcast(I32))
                 for q in range(P // QUADRANT):
-                    nc.sync.dma_start(
+                    nc.gpsimd.dma_start(
                         out=w_exps[QUADRANT * q : QUADRANT * q + 4, :].bitcast(I32),
                         in_=w_scales[0, 4 * q : 4 * q + 4, :].bitcast(I32),
                     )
@@ -75,10 +75,11 @@ def tile_attend_gvq_r_x_kernel(tc, zT, cb, cb2, w_words, w_scales, offs, offs2, 
         both = keep.tile([P, LANES, T], F32, name="both")
         scaled_all = keep.tile([P, LANES, T], F32, name="scaled")
         scaled = [scaled_all[:, :, 0:HALF], scaled_all[:, :, HALF:T]]
-        second = [[keep.tile([P, HALF], F32, name="second%d_%d" % (j, h))[:] if (j, h) != (2, 0) else None for h in range(2)] for j in range(last)]
-        second[2][0] = scaled_all[:, 1, 0:HALF]
-        late = keep.tile([P, CHUNK], F32, name="late")[:]
-        second_last = [late, scaled_all[:, 2, T - CHUNK : T]] + [keep.tile([P, CHUNK], F32, name="second3_c%d" % c)[:] for c in (2, 3)]
+        second = [[keep.tile([P, HALF], F32, name="second%d_%d" % (j, h))[:] if (j, h) != (2, 1) else None for h in range(2)] for j in range(last)]
+        reused = keep.tile([P, HALF], F32, name="reused", align_bytes=64)
+        late = reused[:, CHUNK:HALF]
+        second_last = [reused[:, middle : middle + CHUNK], scaled_all[:, 2, T - CHUNK : T], keep.tile([P, CHUNK], F32, name="second3_c2")[:], reused[:, 0:CHUNK]]
+        second[2][1] = scaled_all[:, 1, 0:HALF]
         first_late = keep.tile([P, HALF], F32, name="first_late")[:]
 
         def entries(codes, t0, t1):
@@ -112,18 +113,20 @@ def tile_attend_gvq_r_x_kernel(tc, zT, cb, cb2, w_words, w_scales, offs, offs2, 
                 on_scalar(second[j][h], book2[j], code2, h * HALF, (h + 1) * HALF, 1.0)
             for h in range(2):
                 on_vector(j, h * HALF, (h + 1) * HALF)
-        scale_on_vector(1, 0, T)
-        for c in range(CHUNKS):
-            on_scalar(second_last[c], book2[last], code2, c * CHUNK, (c + 1) * CHUNK, 1.0 if c < CHUNKS - 1 else -BETA)
+        for c in range(CHUNKS - 1):
+            on_scalar(second_last[c], book2[last], code2, c * CHUNK, (c + 1) * CHUNK, 1.0)
+        scale_on_scalar(1, last, 0, CHUNK)
         for c in range(CHUNKS - 1):
             on_vector(last, c * CHUNK, (c + 1) * CHUNK)
-        scale_on_scalar(2, LANES, 0, CHUNK)
+        scale_on_scalar(last, LANES, 0, CHUNK)
+        on_scalar(second_last[CHUNKS - 1], book2[last], code2, T - CHUNK, T, -BETA)
         on_scalar(late, book[last], code, T - CHUNK, T, -BETA)
-        scale_on_scalar(2, LANES, CHUNK, HALF)
-        scale_on_scalar(2, LANES, HALF, HALF + CHUNK)
-        scale_on_scalar(2, last, T - CHUNK, T)
+        scale_on_scalar(1, LANES, CHUNK, HALF)
+        scale_on_scalar(1, LANES, HALF, HALF + CHUNK)
+        scale_on_scalar(1, last, T - CHUNK, T)
 
-        g_bf = [keep.tile([P, CHUNK, LANES], BF16, name="g_bf%d" % c, align_bytes=64)[:] for c in range(CHUNKS)]
+        g_bf = [keep.tile([P, CHUNK, LANES], BF16, name="g_bf%d" % c, align_bytes=64)[:] if c != 1 else None for c in range(CHUNKS)]
+        g_bf[1] = reused[:].bitcast(BF16).rearrange("p (t j) -> p t j", j=LANES)
         g_codes = [keep.tile([P, CHUNK], U32, name="g_codes%d" % c, align_bytes=64) for c in range(CHUNKS)]
         g_exps = [keep.tile([P, CHUNK], U8, name="g_exps%d" % c, align_bytes=64) for c in range(CHUNKS)]
 
@@ -182,6 +185,9 @@ def tile_attend_gvq_r_x_kernel(tc, zT, cb, cb2, w_words, w_scales, offs, offs2, 
             for m in range(PAIR):
                 acc = psum.tile([P, CHUNK], F32, name=names[m0 + m])
                 product(acc[:], m0 + m, c)
-                copy = nc.vector.tensor_copy if m == 0 else nc.scalar.copy
+                copy = nc.vector.tensor_copy if m == 0 or m0 > 0 else nc.scalar.copy
                 copy(out=result[:, m, :], in_=acc[:])
-            nc.sync.dma_start(out=out_blocks[:, m0 : m0 + PAIR, c * CHUNK : T], in_=result[:])
+                if m0 > 0:
+                    nc.sync.dma_start(out=out_blocks[:, m0 + m, c * CHUNK : T], in_=result[:, m, :])
+            if m0 == 0:
+                nc.sync.dma_start(out=out_blocks[:, m0 : m0 + PAIR, c * CHUNK : T], in_=result[:])

@@ -75,12 +75,11 @@ def tile_attend_gvq_r_x_kernel(tc, zT, cb, cb2, w_words, w_scales, offs, offs2, 
         both = keep.tile([P, LANES, T], F32, name="both")
         scaled_all = keep.tile([P, LANES, T], F32, name="scaled")
         scaled = [scaled_all[:, :, 0:HALF], scaled_all[:, :, HALF:T]]
-        second = [[keep.tile([P, HALF], F32, name="second%d_%d" % (j, h))[:] if (j, h) != (2, 1) else None for h in range(2)] for j in range(last)]
+        second = [[keep.tile([P, HALF], F32, name="second%d_%d" % (j, h))[:] if j > 0 and (j, h) != (2, 1) else None for h in range(2)] for j in range(last)]
         reused = keep.tile([P, HALF], F32, name="reused", align_bytes=64)
         late = reused[:, CHUNK:HALF]
         second_last = [reused[:, middle : middle + CHUNK], scaled_all[:, 2, T - CHUNK : T], keep.tile([P, CHUNK], F32, name="second3_c2")[:], reused[:, 0:CHUNK]]
         second[2][1] = scaled_all[:, 1, 0:HALF]
-        first_late = keep.tile([P, HALF], F32, name="first_late")[:]
 
         def entries(codes, t0, t1):
             return codes[:, t0 // PER_COLUMN : t1 // PER_COLUMN]
@@ -96,33 +95,30 @@ def tile_attend_gvq_r_x_kernel(tc, zT, cb, cb2, w_words, w_scales, offs, offs2, 
         def scale_on_scalar(j0, j1, t0, t1):
             nc.scalar.activation(out=scaled_all[:, j0:j1, t0:t1], in_=both[:, j0:j1, t0:t1], func=COPY, scale=neg_beta[:])
 
-        def scale_on_vector(j, t0, t1):
-            nc.vector.tensor_scalar(out=scaled_all[:, j, t0:t1], in0=both[:, j, t0:t1], scalar1=-BETA, scalar2=None, op0=MULT)
-
-        def add_late(j, values):
-            nc.vector.tensor_tensor(scaled[1][:, j, :], values, second[j][1], ADD)
-
-        nc.vector.tensor_copy(out=second[0][0], in_=book2[0][:].indirect(entries(code2, 0, HALF)))
-        on_scalar(second[0][1], book2[0], code2, HALF, T, -BETA)
-        on_scalar(first_late, book[0], code, HALF, T, -BETA)
-        on_vector(0, 0, HALF)
-        add_late(0, first_late)
-        scale_on_vector(0, 0, HALF)
-        for j in (1, 2):
+        lane0 = keep.tile([P, T], F32, name="lane0")
+        first_late = keep.tile([P, CHUNK], F32, name="first_late")
+        tail = T - CHUNK
+        nc.vector.tensor_copy(out=lane0[:, 0:HALF], in_=book2[0][:].indirect(entries(code2, 0, HALF)))
+        on_scalar(lane0[:, HALF:tail], book2[0], code2, HALF, tail, 1.0)
+        on_scalar(lane0[:, tail:T], book2[0], code2, tail, T, -BETA)
+        on_scalar(first_late[:], book[0], code, tail, T, -BETA)
+        nc.vector.tensor_tensor(both[:, 0, 0:tail], book[0][:].indirect(entries(code, 0, tail)), lane0[:, 0:tail], ADD)
+        nc.vector.tensor_tensor(scaled_all[:, 0, tail:T], first_late[:], lane0[:, tail:T], ADD)
+        for j in range(1, last):
             for h in range(2):
                 on_scalar(second[j][h], book2[j], code2, h * HALF, (h + 1) * HALF, 1.0)
             for h in range(2):
                 on_vector(j, h * HALF, (h + 1) * HALF)
         for c in range(CHUNKS - 1):
             on_scalar(second_last[c], book2[last], code2, c * CHUNK, (c + 1) * CHUNK, 1.0)
-        scale_on_scalar(1, last, 0, CHUNK)
+        scale_on_scalar(0, last, 0, CHUNK)
         for c in range(CHUNKS - 1):
             on_vector(last, c * CHUNK, (c + 1) * CHUNK)
         scale_on_scalar(last, LANES, 0, CHUNK)
         on_scalar(second_last[CHUNKS - 1], book2[last], code2, T - CHUNK, T, -BETA)
         on_scalar(late, book[last], code, T - CHUNK, T, -BETA)
-        scale_on_scalar(1, LANES, CHUNK, HALF)
-        scale_on_scalar(1, LANES, HALF, HALF + CHUNK)
+        scale_on_scalar(0, LANES, CHUNK, HALF)
+        scale_on_scalar(0, LANES, HALF, HALF + CHUNK)
         scale_on_scalar(1, last, T - CHUNK, T)
 
         g_bf = [keep.tile([P, CHUNK, LANES], BF16, name="g_bf%d" % c, align_bytes=64)[:] if c != 1 else None for c in range(CHUNKS)]

@@ -98,15 +98,20 @@ def tile_attend_gvq_r_x_kernel(tc, zT, cb, cb2, w_words, w_scales, offs, offs2, 
         lane0 = keep.tile([P, T], F32, name="lane0")
         first_late = keep.tile([P, CHUNK], F32, name="first_late")
         tail = T - CHUNK
-        nc.vector.tensor_copy(out=lane0[:, 0:HALF], in_=book2[0][:].indirect(entries(code2, 0, HALF)))
+        for t0 in (0, CHUNK):
+            nc.vector.tensor_copy(out=lane0[:, t0 : t0 + CHUNK], in_=book2[0][:].indirect(entries(code2, t0, t0 + CHUNK)))
         on_scalar(lane0[:, HALF:tail], book2[0], code2, HALF, tail, 1.0)
         on_scalar(lane0[:, tail:T], book2[0], code2, tail, T, -BETA)
         on_scalar(first_late[:], book[0], code, tail, T, -BETA)
-        nc.vector.tensor_tensor(both[:, 0, 0:tail], book[0][:].indirect(entries(code, 0, tail)), lane0[:, 0:tail], ADD)
+        for t0, t1 in ((0, CHUNK), (CHUNK, tail)):
+            nc.vector.tensor_tensor(both[:, 0, t0:t1], book[0][:].indirect(entries(code, t0, t1)), lane0[:, t0:t1], ADD)
         nc.vector.tensor_tensor(scaled_all[:, 0, tail:T], first_late[:], lane0[:, tail:T], ADD)
         for j in range(1, last):
-            for h in range(2):
-                on_scalar(second[j][h], book2[j], code2, h * HALF, (h + 1) * HALF, 1.0)
+            spare = middle if j == 1 else 0
+            on_scalar(second[j][0], book2[j], code2, 0, HALF, 1.0)
+            on_scalar(second[j][1][:, 0 : HALF - spare], book2[j], code2, HALF, T - spare, 1.0)
+            if spare:
+                nc.vector.tensor_copy(out=second[j][1][:, HALF - spare : HALF], in_=book2[j][:].indirect(entries(code2, T - spare, T)))
             for h in range(2):
                 on_vector(j, h * HALF, (h + 1) * HALF)
         for c in range(CHUNKS - 1):

@@ -67,7 +67,7 @@ def tile_attend_gvq_r_x_kernel(tc, zT, cb, cb2, w_words, w_scales, offs, offs2, 
             if c == 0:
                 nc.sync.dma_start(out=w_codes[:].bitcast(I32), in_=w_words[0].bitcast(I32))
                 for q in range(P // QUADRANT):
-                    nc.gpsimd.dma_start(
+                    nc.sync.dma_start(
                         out=w_exps[QUADRANT * q : QUADRANT * q + 4, :].bitcast(I32),
                         in_=w_scales[0, 4 * q : 4 * q + 4, :].bitcast(I32),
                     )

from contextlib import ExitStack

import concourse.mybir as mybir

N_FEAT, T, C, D = 512, 512, 512, 512
BETA = 0.25
FLOPS = 2 * N_FEAT * D * T

F32 = mybir.dt.float32
BF16 = mybir.dt.bfloat16
I32 = mybir.dt.int32
U32 = mybir.dt.uint32
U16 = mybir.dt.uint16
U8 = mybir.dt.uint8
E5M2X4 = mybir.dt.float8_e5m2_x4
E2M1X4 = mybir.dt.float4_e2m1fn_x4
ADD = mybir.AluOpType.add
MULT = mybir.AluOpType.mult
COPY = mybir.ActivationFunctionType.Copy

P = 128
LANES = 4
PER_COLUMN = 16
HALF = T // 2
CHUNK = 128
CHUNKS = T // CHUNK
PAIR = 2
QUADRANT = 32


def tile_attend_gvq_r_x_kernel(tc, zT, cb, cb2, w_words, w_scales, offs, offs2, out):
    nc = tc.nc
    z_lanes = zT.rearrange("(p j) t -> p j t", j=LANES)
    cb_lanes = cb.rearrange("(p j) c -> p j c", j=LANES)
    cb2_lanes = cb2.rearrange("(p j) c -> p j c", j=LANES)
    out_blocks = out.rearrange("(m p) t -> p m t", p=P)
    last = LANES - 1
    middle = CHUNK // 2

    with ExitStack() as ctx:
        keep = ctx.enter_context(tc.tile_pool(name="keep", bufs=1))
        psum = ctx.enter_context(tc.psum_pool(name="psum", bufs=1))

        code = keep.tile([P, T // PER_COLUMN], U16, name="code")
        code2 = keep.tile([P, T // PER_COLUMN], U16, name="code2")
        book = [keep.tile([P, C], F32, name="book%d" % j) for j in range(LANES)]
        book2 = [keep.tile([P, C], F32, name="book2_%d" % j) for j in range(LANES)]
        z = [keep.tile([P, LANES, CHUNK], F32, name="z%d" % c)[:] for c in range(CHUNKS)]
        w_codes = keep.tile([P, 2 * D], U8, name="w_codes", align_bytes=64)
        w_exps = keep.tile([P, D], U8, name="w_exps", align_bytes=64)

        ones = keep.tile([P, 1], F32, name="ones")
        neg_beta = keep.tile([P, 1], F32, name="neg_beta")
        nc.gpsimd.memset(ones[:], 1.0)
        nc.scalar.activation(out=neg_beta[:], in_=ones[:], func=COPY, scale=-BETA)
        nc.gpsimd.memset(w_exps[:].bitcast(U32), 0)

        nc.sync.dma_start(out=book2[0][:], in_=cb2_lanes[:, 0, :])
        nc.sync.dma_start(code2[:], offs2)
        nc.sync.dma_start(out=book[0][:], in_=cb_lanes[:, 0, :])
        nc.sync.dma_start(code[:], offs)
        for j in range(1, LANES):
            nc.sync.dma_start(out=book2[j][:], in_=cb2_lanes[:, j, :])
            nc.sync.dma_start(out=book[j][:], in_=cb_lanes[:, j, :])
        for c in range(CHUNKS):
            nc.sync.dma_start(out=z[c], in_=z_lanes[:, :, c * CHUNK : (c + 1) * CHUNK])
            if c == 0:
                nc.sync.dma_start(out=w_codes[:].bitcast(I32), in_=w_words[0].bitcast(I32))
                for q in range(P // QUADRANT):
                    nc.sync.dma_start(
                        out=w_exps[QUADRANT * q : QUADRANT * q + 4, :].bitcast(I32),
                        in_=w_scales[0, 4 * q : 4 * q + 4, :].bitcast(I32),
                    )

        both = keep.tile([P, LANES, T], F32, name="both")
        scaled_all = keep.tile([P, LANES, T], F32, name="scaled")
        scaled = [scaled_all[:, :, 0:HALF], scaled_all[:, :, HALF:T]]
        second = [[keep.tile([P, HALF], F32, name="second%d_%d" % (j, h))[:] if j > 0 and (j, h) != (2, 1) else None for h in range(2)] for j in range(last)]
        reused = keep.tile([P, HALF], F32, name="reused", align_bytes=64)
        late = reused[:, CHUNK:HALF]
        second_last = [reused[:, middle : middle + CHUNK], scaled_all[:, 2, T - CHUNK : T], keep.tile([P, CHUNK], F32, name="second3_c2")[:], reused[:, 0:CHUNK]]
        second[2][1] = scaled_all[:, 1, 0:HALF]

        def entries(codes, t0, t1):
            return codes[:, t0 // PER_COLUMN : t1 // PER_COLUMN]

        def on_vector(j, t0, t1):
            h, a0 = divmod(t0, HALF)
            other = second_last[t0 // CHUNK] if j == last else second[j][h][:, a0 : a0 + t1 - t0]
            nc.vector.tensor_tensor(both[:, j, t0:t1], book[j][:].indirect(entries(code, t0, t1)), other, ADD)

        def on_scalar(place, window, codes, t0, t1, factor):
            nc.scalar.activation(out=place, in_=window[:].indirect(entries(codes, t0, t1)), func=COPY, scale=factor)

        def scale_on_scalar(j0, j1, t0, t1):
            nc.scalar.activation(out=scaled_all[:, j0:j1, t0:t1], in_=both[:, j0:j1, t0:t1], func=COPY, scale=neg_beta[:])

        lane0 = keep.tile([P, T], F32, name="lane0")
        first_late = keep.tile([P, CHUNK], F32, name="first_late")
        tail = T - CHUNK
        for t0 in (0, CHUNK):
            nc.vector.tensor_copy(out=lane0[:, t0 : t0 + CHUNK], in_=book2[0][:].indirect(entries(code2, t0, t0 + CHUNK)))
        on_scalar(lane0[:, HALF:tail], book2[0], code2, HALF, tail, 1.0)
        on_scalar(lane0[:, tail:T], book2[0], code2, tail, T, -BETA)
        on_scalar(first_late[:], book[0], code, tail, T, -BETA)
        for t0, t1 in ((0, CHUNK), (CHUNK, tail)):
            nc.vector.tensor_tensor(both[:, 0, t0:t1], book[0][:].indirect(entries(code, t0, t1)), lane0[:, t0:t1], ADD)
        nc.vector.tensor_tensor(scaled_all[:, 0, tail:T], first_late[:], lane0[:, tail:T], ADD)
        for j in range(1, last):
            spare = middle if j == 1 else 0
            on_scalar(second[j][0], book2[j], code2, 0, HALF, 1.0)
            on_scalar(second[j][1][:, 0 : HALF - spare], book2[j], code2, HALF, T - spare, 1.0)
            if spare:
                nc.vector.tensor_copy(out=second[j][1][:, HALF - spare : HALF], in_=book2[j][:].indirect(entries(code2, T - spare, T)))
            for h in range(2):
                on_vector(j, h * HALF, (h + 1) * HALF)
        for c in range(CHUNKS - 1):
            on_scalar(second_last[c], book2[last], code2, c * CHUNK, (c + 1) * CHUNK, 1.0)
        scale_on_scalar(0, last, 0, CHUNK)
        for c in range(CHUNKS - 1):
            on_vector(last, c * CHUNK, (c + 1) * CHUNK)
        scale_on_scalar(last, LANES, 0, CHUNK)
        on_scalar(second_last[CHUNKS - 1], book2[last], code2, T - CHUNK, T, -BETA)
        on_scalar(late, book[last], code, T - CHUNK, T, -BETA)
        scale_on_scalar(0, LANES, CHUNK, HALF)
        scale_on_scalar(0, LANES, HALF, HALF + CHUNK)
        scale_on_scalar(1, last, T - CHUNK, T)

        g_bf = [keep.tile([P, CHUNK, LANES], BF16, name="g_bf%d" % c, align_bytes=64)[:] if c != 1 else None for c in range(CHUNKS)]
        g_bf[1] = reused[:].bitcast(BF16).rearrange("p (t j) -> p t j", j=LANES)
        g_codes = [keep.tile([P, CHUNK], U32, name="g_codes%d" % c, align_bytes=64) for c in range(CHUNKS)]
        g_exps = [keep.tile([P, CHUNK], U8, name="g_exps%d" % c, align_bytes=64) for c in range(CHUNKS)]

        def gradient(c, a0, a1):
            h, t0 = divmod(c * CHUNK, HALF)
            nc.vector.scalar_tensor_tensor(
                out=g_bf[c][:, a0:a1, :],
                in0=z[c][:, :, a0:a1].rearrange("p j t -> p t j"),
                scalar=BETA,
                in1=scaled[h][:, :, t0 + a0 : t0 + a1].rearrange("p j t -> p t j"),
                op0=MULT,
                op1=ADD,
            )

        def quantise(c, a0, a1):
            nc.vector.quantize_mx(
                out=g_codes[c][:, a0:a1].bitcast(E5M2X4),
                scales=g_exps[c][:, a0:a1],
                in_=g_bf[c][:, a0:a1, :].rearrange("p t j -> p (t j)"),
            )

        def product(acc, m, c):
            nc.tensor.matmul_mx(
                out=acc,
                lhsT=w_codes[:, 2 * P * m : 2 * P * (m + 1)].bitcast(E2M1X4),
                lhsT_scale=w_exps[:, P * m : P * (m + 1)],
                rhs=g_codes[c][:].bitcast(E5M2X4),
                rhs_scale=g_exps[c][:],
                start=True,
                stop=True,
            )

        gradient(0, 0, CHUNK)
        nc.vector.tensor_tensor(scaled_all[:, last, T - CHUNK : T], late, second_last[CHUNKS - 1], ADD)
        quantise(0, 0, CHUNK)
        gradient(1, 0, CHUNK)
        for c in range(2, CHUNKS):
            gradient(c, 0, middle)
            quantise(c - 1, 0, CHUNK)
            gradient(c, middle, CHUNK)
        quantise(3, 0, middle)
        quantise(3, middle, CHUNK)

        for c in range(CHUNKS - 1):
            for m0 in (0, PAIR):
                acc = psum.tile([P, PAIR, CHUNK], F32, name="acc%d_%d" % (c, m0))
                for m in range(PAIR):
                    product(acc[:, m, :], m0 + m, c)
                result = keep.tile([P, PAIR, CHUNK], F32, name="result%d_%d" % (c, m0))[:]
                nc.scalar.copy(out=result, in_=acc[:])
                nc.sync.dma_start(out=out_blocks[:, m0 : m0 + PAIR, c * CHUNK : (c + 1) * CHUNK], in_=result)
        c = CHUNKS - 1
        names = ["acc3_0", "acc3_2", "acc0_0", "acc0_2"]
        for m0 in (0, PAIR):
            result = keep.tile([P, PAIR, CHUNK], F32, name="result3_%d" % m0)
            for m in range(PAIR):
                acc = psum.tile([P, CHUNK], F32, name=names[m0 + m])
                product(acc[:], m0 + m, c)
                copy = nc.vector.tensor_copy if m == 0 or m0 > 0 else nc.scalar.copy
                copy(out=result[:, m, :], in_=acc[:])
                if m0 > 0:
                    nc.sync.dma_start(out=out_blocks[:, m0 + m, c * CHUNK : T], in_=result[:, m, :])
            if m0 == 0:
                nc.sync.dma_start(out=out_blocks[:, m0 : m0 + PAIR, c * CHUNK : T], in_=result[:])
